import numpy as np, ml_dtypes
CORES = [2,6,10,14,18,22,26,30]
N = 8
BF = ml_dtypes.bfloat16
V, D, L, RO, HOP = 2048, 8, 256, 3, 3
def meet(rng, n, rest):
    p = np.argsort(rng.random((N, 8, n, V)), axis=-1); h = np.zeros_like(p)
    np.put_along_axis(h, p[..., 0::2], p[..., 1::2], 3); np.put_along_axis(h, p[..., 1::2], p[..., 0::2], 3)
    o = np.concatenate([h, rest], axis=2)
    return np.ascontiguousarray(np.take_along_axis(o, np.argsort(rng.random(o.shape), axis=2), 2))
def court(rng, lo, hi):
    c = rng.integers(0, V, (N, 8, V))
    for r in range(N):
        for g in range(8):
            h = int(rng.integers(3, 10)); chief = rng.permutation(V)[:h]; w = np.add.accumulate(np.exp2(-(0.1 + rng.random()) * np.arange(h)))
            j = np.minimum(np.searchsorted(w, rng.random(V) * w[-1], side="right"), h - 1)
            c[r, g] = np.where(rng.random(V) < lo + (hi - lo) * rng.random(), chief[j], c[r, g])
    return c
def hubs(rng, og, n):
    z = rng.permutation(V)[:RO * n]; vv = np.concatenate([D * rng.permutation(L)[:16 * n] + t for t in range(RO)]).reshape(RO * n, 16)
    og[rng.integers(0, 16, vv.shape), vv] = z[:, None]; og[:, z] = vv.T
    return z
def pack(o, x, c):
    return {"hol": np.ascontiguousarray(o.reshape(N, 128, V)).astype(np.int32), "sha": np.ascontiguousarray(x.reshape(N, 128, V)).astype(np.float32).astype(BF), "ctl": c.astype(np.int32)}
def setup_inputs(rng):
    o = meet(rng, 8, rng.integers(0, V, (N, 8, 8, V))); c = court(rng, 0.85, 0.95); x = rng.integers(0, 16, (N, 8, 16, V))
    for r in range(N):
        for g in range(8): hubs(rng, o[r, g], 2)
    return pack(o, x, c)
def setup_inputs_spread(rng):
    e = rng.integers(1, 7, (N, 8, 1, 1)); o = meet(rng, 8, np.minimum((V * rng.random((N, 8, 8, V)) ** e).astype(np.int64), V - 1))
    c = court(rng, 0.5, 1.0); q = np.minimum((V * rng.random((N, 8, V)) ** rng.integers(1, 9, (N, 8, 1))).astype(np.int64), V - 1)
    c = np.where(rng.random((N, 8, V)) < 0.15, q, c)
    x = np.minimum((rng.random((N, 8, 16, V)) * rng.choice(np.array([1, 2, 3, 6, 11, 16]), (N, 8, 1, V))).astype(np.int64), 15)
    return pack(o, x, c)
def setup_inputs_ends(rng):
    top = V - 1; p = rng.choice(np.array([0.15, 0.5, 0.85]), (N, 8, 1, V)); odd = np.arange(16) % 2
    o = meet(rng, 6, np.where(rng.random((N, 8, 10, V)) < p, top, 0)); c = top * rng.integers(0, 2, (N, 8, V)); kind = rng.random((N, 8, 1, V))
    x = 15 * np.where(kind < 0.45, 1, np.where(kind < 0.55, 0, rng.integers(0, 2, (N, 8, 16, V))))
    for r in range(N):
        for g in range(8):
            og, xg, cg = o[r, g], x[r, g], c[r, g]
            if g % 4 == 1: cg[0] = top; cg[top] = 0
            elif g % 4 != 3 or g == 7:
                cg[0] = 0; cg[top] = top; xg[:, 0] = 15; xg[:, top] = 15; og[:, 0] = top * odd
                for t in range(RO):
                    v = D * (L - 1) + t; og[:, v] = top; xg[:, v] = 15
                    v = D * (L - 2) + t; og[:, v] = top * odd; xg[:, v] = 15
                    v = D + t; og[:, v] = top * (1 - odd); xg[:, v] = 15
                    xg[:, 2 * D + t] = 0
                    v = D * (L - 3) + t; z = D * (L - 1 - 2 * t) + D - 2; og[:, v] = top; xg[:, v] = 15
                    for k, a in ((14, z), (15, z - D)): og[k, v] = a; og[15, a] = v; xg[:, a] = 0; cg[a] = 0
    return pack(o, x, c)
def setup_inputs_corners(rng):
    o = meet(rng, 8, rng.integers(0, V, (N, 8, 8, V))); c = court(rng, 0.8, 1.0); x = rng.integers(0, 16, (N, 8, 16, V)); own = np.arange(V)
    kind = rng.integers(0, 8, (N, 8, 1, V)); x = np.where(kind == 0, 0, np.where(kind == 1, 15, x))
    for r in range(N):
        mo, ho = rng.permutation(8), rng.permutation(8)
        for g in range(8):
            og = o[r, g]; m, h = int(mo[g]), int(ho[g])
            if m == 0: c[r, g] = own
            elif m == 1: c[r, g] = 0
            elif m == 2: c[r, g] = V - 1
            elif m == 3: c[r, g] = (own + 1) % V
            elif m == 4: c[r, g] = V - 1 - own
            elif m == 5: c[r, g] = np.choose(rng.integers(0, 3, V), [np.zeros_like(own), own, np.full_like(own, V - 1)])
            if h in (0, 4): og[rng.integers(0, 16, V), own] = own
            elif h == 1: one = rng.random(V) < 0.3; og[:, one] = og[:1, one]
            elif h == 2: og[:] = np.choose(rng.integers(0, 3, (16, V)), [np.zeros((16, V), np.int64), np.broadcast_to(own, (16, V)), np.full((16, V), V - 1)])
            elif h == 3: og[3] = (own + 1) % V; og[12] = (own - 1) % V
    return pack(o, x, c)
def setup_inputs_ties(rng):
    o = meet(rng, 8, rng.integers(0, V, (N, 8, 8, V))); x = rng.integers(14, 16, (N, 8, 16, V)); c = np.zeros((N, 8, V), np.int64); idle = np.flatnonzero(np.arange(V) % D >= RO)
    for g in range(8):
        f = rng.permutation(idle)[:3]; f = f[:2 + g % 2]
        for r in range(N):
            c[r, g] = f[rng.integers(0, 2, V)]
            if g % 2: c[r, g] = np.where(rng.random(V) < 0.1, f[2], c[r, g])
            c[r, g, f] = f
            if g % 4 == 1: x[r, g] = 15
            elif g % 4 == 2:
                n = 9 if g == 2 else int(rng.integers(8, 11)); x[r, g] = (rng.permutation(16) < n).astype(np.int64)[:, None] * rng.integers(1, 16, (16, 1))
            elif g % 4 == 3: x[r, g] -= 7
    return pack(o, x, c)
def setup_inputs_rush(rng):
    o = meet(rng, 8, rng.integers(0, V, (N, 8, 8, V))); x = rng.integers(6, 16, (N, 8, 16, V)); low = rng.integers(0, 4, (N, 8, 16, V)); c = np.zeros((N, 8, V), np.int64)
    act, idle = np.flatnonzero(np.arange(V) % D < RO), np.flatnonzero(np.arange(V) % D >= RO)
    for g in range(8):
        f = rng.permutation(idle)[:2]; tp = {5: 0, 7: RO - 1}.get(g, -1)
        if tp >= 0: f[0] = D * int(rng.integers(0, L)) + tp
        for r in range(N):
            og = o[r, g]; k = rng.integers(0, 16, V); c[r, g] = np.where(rng.random(V) < 0.8, f[0], f[1]); z = act
            if g % 4 == 0: z = hubs(rng, og, L // 16)
            elif g % 4 == 1:
                for t in range(RO):
                    q = D * rng.permutation(L) + t; a, b = q[0::2], q[1::2]; og[k[a], a] = b; og[k[b], b] = a
            elif g % 4 == 2:
                og[k[act], act] = act; h = act[rng.random(len(act)) < 0.5]; og[(k[h] + 5) % 16, h] = h
            else:
                n = min(len(act), len(idle)); a, z = rng.permutation(act)[:n], rng.permutation(idle)[:n]
                for j in range(5): og[(k[a] + j) % 16, a] = z; og[(k[z] + j) % 16, z] = a
            c[r, g, z] = f[1]; x[r, g][:, z] = low[r, g][:, z]
            c[r, g, f] = f; x[r, g][:, f[0]] = 15
            if tp >= 0:
                h, y = [int(e) for e in rng.permutation(idle[idle != f[1]])[:2]]; i1, i2 = [int(e) for e in rng.permutation(16)[:2]]
                v = D * ((int(f[0]) // D + 1 + int(rng.integers(0, L - 1))) % L) + tp
                og[:, v] = h; og[i1, v] = f[0]; og[i2, v] = y; og[int(rng.integers(0, 16)), y] = v
                og[:, f[0]] = h; og[int(rng.integers(0, 16)), f[0]] = v
                c[r, g, h] = f[0]; c[r, g, v] = f[1]; c[r, g, y] = f[1]; x[r, g][:, h] = 15; x[r, g][:, v] = rng.integers(1, 4, 16)
    return pack(o, x, c)
def check_inputs(d):
    bad = []
    for k, hi in (("hol", V - 1), ("sha", 15), ("ctl", V - 1)):
        v = np.asarray(d[k]).astype(np.float64)
        if not (np.min(v) >= 0 and np.max(v) <= hi): bad.append("range of " + k)
        elif np.any(v != np.floor(v)): bad.append("whole numbers of " + k)
    return bad
def reference(hol, sha, ctl):
    o = hol.astype(np.int64).reshape(N, 8, 16, V); x = sha.astype(np.float32).astype(np.int64).reshape(N, 8, 16, V); c = ctl.astype(np.int64)
    last = np.zeros(N, np.int64)
    for t in range(RO):
        d = 1 + t % (N - 1); vs = D * np.arange(L) + t
        no, nc, wins = [], [], []
        for r in range(N):
            a = o[r][:, :, vs]; af = a.reshape(8, 16 * L); cf = af
            for h in range(HOP): cf = np.take_along_axis(c[(r + h * d) % N], cf, 1)
            ck = cf.reshape(8, 16, L)
            xk = np.take_along_axis(x[r], af[:, None, :], 2).reshape(8, 16, 16, L); xv = x[r][:, :, vs]
            m = np.add.reduce(np.minimum(xk, xv[:, :, None, :]), axis=1)
            pool = np.add.reduce(np.where(ck[:, :, None, :] == ck[:, None, :, :], m[:, None, :, :], 0), axis=2)
            kb = np.argmax(pool, axis=1)
            b = np.take_along_axis(ck, kb[:, None, :], 1)[:, 0]
            mine = ck == b[:, None, :]
            part = np.add.reduce(np.where(mine[:, None, :, :], xk, 0), axis=2); full = np.add.reduce(xk, axis=2)
            win = np.add.reduce((2 * part > full).astype(np.int64), axis=1) >= 9 + (last[r] & 1)
            ok = np.take_along_axis(o[r], af[:, None, :], 2).reshape(8, 16, 16, L)
            stake = np.any(ok == vs, axis=1)
            xb = np.take_along_axis(x[r], b[:, None, :], 2)
            far = np.where(stake & ~mine, np.add.reduce(np.abs(xk - xb[:, :, None, :]), axis=1), -1)
            ks = np.argmax(far, axis=1); sells = win & (np.max(far, axis=1) >= 0)
            goal = np.take_along_axis(a, ks[:, None, :], 1)[:, 0]; cs = np.take_along_axis(ck, ks[:, None, :], 1)[:, 0]
            on = o[r] + 0; cn = c[r] + 0
            for g in range(8):
                ln = np.flatnonzero(sells[g]); tg, first = np.unique(goal[g, ln], return_index=True); w = ln[first]
                col = o[r, g][:, tg]; on[g][:, tg] = np.where(col == vs[w], cs[g, w], col)
                on[g, ks[g, ln], vs[ln]] = b[g, ln]
            cn[:, vs] = np.where(win, b, vs)
            no.append(on); nc.append(cn); wins.append(np.add.reduce(win.astype(np.int64).reshape(-1)))
        o = np.stack(no); c = np.stack(nc); last = np.array(wins, np.int64)
    return {"yo": o.reshape(N, 128, V).astype(np.float32), "yc": c.astype(np.float32)}

@@ -1,0 +1,686 @@
+import numpy as np
+from concourse.mybir import AluOpType as A, ActivationFunctionType as F, AxisListType
+from concourse.bass import DstId, RemoteDMATransfer
+
+V, D, L, RO, N = 2048, 8, 256, 3, 8
+DEL = (1, 2, 4, 3, 6)
+NEXT = {0: (2, 4, 3, 6), 1: (3, 6)}
+NV = {"min": 7, "win": 5, "far": 4}
+S_ = np.s_
+
+_bf, _f, _i, _u = "bfloat16", "float32", "int32", "uint16"
+_shapes = {
+    "O": ([2304], _f), "holI": ([2048], _i), "X": ([2048], _bf), "raw": ([128], _i), "rawd": ([128], _f),
+    "HL": ([256], _bf), "VV": ([4096], _f), "xk": ([4096], _bf), "sk": ([4096], _bf), "dR": ([4096], _bf),
+    "mR": ([4096], _bf), "pR": ([4096], _bf), "T1": ([2048], _bf), "DT": ([2048], _bf), "EK": ([2048], _bf),
+    "E3": ([16, 272], _bf), "ycS": ([2048], _f),
+    "EQ": ([128, 16], _bf), "PA": ([128, 16], _bf), "PB": ([64, 32], _bf),
+    "off0": ([128], _u), "off1": ([128], _u), "a16": ([256], _u), "bo": ([16], _u), "go": ([16], _u), "so": ([16], _u),
+    "gSu": ([256], _u), "aD": ([256], _f), "cd": ([16, 24], _f), "md": ([16, 24], _bf), "cS": ([256], _f),
+    "keyS": ([256], _f), "mxS": ([256], _f), "keyK": ([256], _f), "mx16": ([128], _f), "oh": ([256], _f), "ohc": ([256], _f),
+    "cK": ([256], _f), "mine": ([256], _bf), "w1": ([256], _bf), "w16": ([256], _bf), "bw": ([256], _f), "bws": ([256], _f),
+    "xb": ([256], _bf), "gt": ([256], _bf), "winG": ([256], _f), "st": ([256], _bf), "el": ([256], _f), "elw": ([256], _f),
+    "FK": ([256], _f), "FKk": ([256], _f), "fS": ([256], _f), "soh": ([256], _f), "ga": ([256], _f), "ca": ([256], _f), "ns": ([256], _f),
+    "sb": ([256], _f), "gw": ([256], _f), "gws": ([256], _f), "OG": ([256], _f), "dw": ([256], _f), "dws": ([256], _f),
+    "t1": ([16], _f), "t2": ([16], _f), "eqv": ([256], _f), "dd": ([256], _f), "tt": ([256], _f), "oc": ([256], _f),
+    "hR": ([256], _bf), "hU": ([256], _f), "vR": ([256], _bf), "vW": ([256], _bf), "vU": ([256], _f),
+    "cnw": ([1], _f), "cni": ([1], _i), "cnp": ([1], _i), "Z": ([1], _f),
+    "IF": ([256], _f), "JG": ([256], _f), "JM": ([256], _f), "JM3": ([16, 16], _f), "pi": ([1], _i), "qi": ([1], _i),
+    "cols": ([16], _f), "I": ([128], _bf), "I16": ([128], _bf), "I256": ([128], _bf), "nI": ([128], _bf), "Iw": ([128], _bf),
+    "I32": ([128], _f), "Blk": ([128], _bf), "Blk32": ([128], _f), "BlkC": ([128], _bf), "B4096": ([128], _bf), "BlkV": ([128], _bf),
+    "fm": ([16, 8], _bf), "Blk8": ([8], _bf), "Blk8c": ([8], _bf), "B8s": ([8], _bf), "B816": ([8], _bf), "B8n32": ([8], _bf),
+    "B8h": ([8], _bf), "B8nh": ([8], _bf), "KSc": ([144], _bf),
+    "km": ([16], _f), "maskW": ([256], _f), "rst": ([256], _f), "tri": ([16, 16], _bf), "E1": ([256], _f), "k15": ([16, 16], _bf),
+    "kc": ([256], _bf), "dumG": ([256], _f), "dumW": ([16], _f), "zer": ([256], _bf), "o16": ([128], _f),
+}
+SCRATCH = {n: ("sbuf", [128] + s, d) for n, (s, d) in _shapes.items()}
+PACK = {n: 256 * j for j, n in enumerate((
+    "aD cS keyS mxS keyK oh ohc cK bw bws el elw winG FK FKk fS soh ga ca ns sb gw gws OG dw dws eqv dd tt oc hU vU").split())}
+SHAPE = dict(SCRATCH)
+for _n in PACK:
+    del SCRATCH[_n]
+SCRATCH["lanes"] = ("sbuf", [128, 256 * len(PACK)], _f)
+for _d in (0,) + DEL:
+    SCRATCH["tab%d" % _d] = ("sbuf", [128, 2048], _bf)
+for _d in DEL:
+    SCRATCH["la%d" % _d] = ("sbuf", [128, 256], _bf)
+for _t in NEXT:
+    for _d in NEXT[_t]:
+        SCRATCH["lb%d%d" % (_t, _d)] = ("sbuf", [128, 256], _bf)
+for _t in range(RO):
+    SCRATCH["CN%d" % _t] = ("sbuf", [128, 256], _bf)
+    SCRATCH["vHL%d" % _t] = ("sbuf", [128, 256], _bf)
+    SCRATCH["vG%d" % _t] = ("sbuf", [128, 256], _f)
+for _k in range(8):
+    SCRATCH["k%d" % _k] = ("psum", [128, 512] if _k in (0, 7) else [128, 16, 32], _f)
+SHAPE.update(SCRATCH)
+SEMAPHORES = ["qv", "qs", "qp", "qg", "ls"] + ["d%d" % k for k in range(24)] + ["a%d" % d for d in DEL] + ["b%d%d" % (t, d) for t in NEXT for d in NEXT[t]]
+
+
+def b(n, *ix):
+    return (n, (slice(None),) + ix)
+
+
+def bp(n, p, *ix):
+    return (n, (p,) + ix)
+
+
+def ind(w, o):
+    return ("ind", w, o)
+
+
+def rank_program(g, core, T, topo):
+    rank = T.rank_of(core)
+    if rank is None:
+        return
+    eng = {"v": g.vector, "s": g.scalar, "p": g.tensor, "g": g, "y": g.sync}
+    cnt, clk, hist, W, R, cache = {}, {q: {} for q in eng}, {}, {}, {}, {}
+    ndma = [0]
+
+    def ap(x):
+        if x[0] == "ind":
+            return T[x[1][0]][x[1][1]].indirect(T[x[2][0]][x[2][1]])
+        if x[0] in PACK:
+            lo, hi, st = (x[1][1] if len(x[1]) > 1 else slice(None)).indices(256)
+            return T["lanes"][x[1][0], PACK[x[0]] + lo:PACK[x[0]] + hi:st]
+        return T[x[0]][x[1]]
+
+    def parts(xs):
+        out = []
+        for x in xs:
+            if isinstance(x, tuple):
+                out += [x[1], x[2]] if x[0] == "ind" else [x]
+        return out
+
+    def size(n):
+        return int(np.prod(SHAPE[n][1][1:]))
+
+    def cols(x):
+        key = repr(x)
+        if key not in cache:
+            ix = x[1][1:]
+            m = np.arange(size(x[0])).reshape(SHAPE[x[0]][1][1:])
+            cache[key] = m[ix].ravel() if ix else m.ravel()
+        return cache[key]
+
+    def need(q, rd, wr):
+        req = {}
+        own = "q" + q
+
+        def take(tab, x, skip):
+            ps = SHAPE[x[0]][0] == "psum"
+            for s, arr in tab.get(x[0], {}).items():
+                if s == own and skip:
+                    continue
+                n = int(arr.max() if ps and s != own else arr[cols(x)].max())
+                if n > req.get(s, 0):
+                    req[s] = n
+        for x in rd:
+            take(W, x, False)
+            if SHAPE[x[0]][0] == "psum":
+                take(R, x, True)
+        for x in wr:
+            take(W, x, True)
+            take(R, x, True)
+        return req
+
+    def waits(q, req):
+        for s, n in sorted(req.items(), key=lambda z: -len(hist.get(z, ()))):
+            if clk[q].get(s, 0) < n:
+                eng[q].wait_ge(T.sem[s], n)
+                clk[q][s] = n
+                for s2, n2 in hist.get((s, n), {}).items():
+                    clk[q][s2] = max(clk[q].get(s2, 0), n2)
+
+    def note(tab, x, s, n):
+        d = tab.setdefault(x[0], {})
+        if s not in d:
+            d[s] = np.zeros(size(x[0]), np.int64)
+        d[s][cols(x)] = n
+
+    def op(q, fn, rd, wr, sem=None, amt=1):
+        rd, wr = parts(rd), parts(wr)
+        waits(q, need(q, rd, wr))
+        s = sem or "q" + q
+        cnt[s] = cnt.get(s, 0) + amt
+        n = cnt[s]
+        fn().then_inc(T.sem[s], amt)
+        hist[(s, n)] = dict(clk[q])
+        if sem is None:
+            hist[(s, n)][s] = n
+        for x in rd:
+            note(R, x, s, n)
+        for x in wr:
+            note(W, x, s, n)
+
+    v, sc, te = g.vector, g.scalar, g.tensor
+
+    def vt(out, i0, i1, o):
+        op("v", lambda: v.tensor_tensor(ap(out), ap(i0), ap(i1), o), [i0, i1] + ([out[2]] if out[0] == "ind" else []), [out[1] if out[0] == "ind" else out])
+
+    def vs(out, i0, s1, o1, s2=None, o2=None):
+        a = [ap(x) if isinstance(x, tuple) else x for x in (s1, s2)]
+        if o2 is None:
+            op("v", lambda: v.tensor_scalar(ap(out), ap(i0), a[0], None, o1), [i0, s1], [out])
+        else:
+            op("v", lambda: v.tensor_scalar(ap(out), ap(i0), a[0], a[1], o1, o2), [i0, s1, s2], [out])
+
+    def vc(out, i):
+        op("v", lambda: v.tensor_copy(ap(out), ap(i)), [i], [out])
+
+    def ms(out, c):
+        op("v", lambda: v.memset(ap(out), c), [], [out])
+
+    def scan(out, d0, d1, o0, o1):
+        op("v", lambda: v.tensor_tensor_scan(ap(out), ap(d0), ap(d1), 0.0, o0, o1), [d0, d1], [out])
+
+    def act(out, i, f=F.Identity, bias=0.0, scale=1.0):
+        a = [ap(x) if isinstance(x, tuple) else x for x in (bias, scale)]
+        op("s", lambda: sc.activation(ap(out), ap(i), f, bias=a[0], scale=a[1]), [i, bias, scale], [out])
+
+    def mm(out, l, r, start, stop):
+        op("p", lambda: te.matmul(ap(out), ap(l), ap(r), bool(start), bool(stop)), [l, r], [out])
+
+    def iota(out, pat, base, cm):
+        kw = {} if SCRATCH[out[0]][2] == _i else {"allow_small_or_imprecise_dtypes": True}
+        op("g", lambda: g.iota(ap(out), pat, base, cm, **kw), [], [out])
+
+    def dma(out, i):
+        s = "d%d" % ndma[0]
+        ndma[0] += 1
+        o_, i_ = (ap(x) if x[0] in SCRATCH else T[x[0]][x[1]] for x in (out, i))
+        op("y", lambda: g.sync.dma_start(o_, i_), [i] if i[0] in SCRATCH else [], [out] if out[0] in SCRATCH else [], s, 16)
+
+    nls = [0]
+
+    def send(src, items, ne):
+        waits("g", need("g", [src], []))
+        tr, k = [], 0
+        for d, dst, sem in items:
+            to = T.cores[(rank - d) % N]
+            rid, pid = topo.addr(to)[:2]
+            es = topo.engines(core, to)[k:k + ne]
+            k += ne
+            tr.append(RemoteDMATransfer(dst_ids=[DstId(rid=rid, pnc=pid)], dma_engine_mask=sum(1 << e for e in es), remote_sem=T.sem[sem], src=ap(src), dst=T[dst][:], alu_op=0))
+            nls[0] += ne
+        g.remote_dma_fused(tr, local_sem=T.sem.ls)
+
+    def arrives(dst, sem, ne):
+        cnt[sem] = ne
+        note(W, b(dst), sem, ne)
+
+    fills = []
+
+    def fill(n=1):
+        for _ in range(n):
+            if fills:
+                fills.pop(0)()
+    full = S_[:]
+    NE = 4
+    dma(b("raw"), ("ctl", S_[:]))
+    dma(b("holI"), ("hol", S_[:]))
+    dma(b("X"), ("sha", S_[:]))
+    iota(b("pi"), [[0, 1]], 0, 1)
+    iota(b("IF"), [[1, 256]], 0, 0)
+    iota(b("JG"), [[1, 16], [0, 16]], 0, 0)
+    iota(b("JM"), [[0, 16], [1, 16]], 0, 0)
+    col = {n: b("cols", S_[j:j + 1]) for j, n in enumerate(("p", "q", "g", "g15", "is", "po", "w", "po2"))}
+    vs(b("qi"), b("pi"), 15, A.bitwise_and)
+    vc(col["p"], b("pi"))
+    vc(col["q"], b("qi"))
+    vt(col["g15"], b("pi"), b("qi"), A.subtract)
+    vs(b("cni"), b("qi"), 1, A.bitwise_and)
+    vs(col["g"], col["g15"], 1.0 / 16, A.mult)
+    vs(col["is"], col["q"], 2.0, A.is_lt)
+    vc(col["po"], b("cni"))
+    vs(col["g15"], col["g15"], 15.0, A.add)
+    ms(b("tab0"), 0.0)
+    vs(b("HL", S_[0:128]), b("raw"), 2048.0, A.add)
+    vt(b("rawd"), b("raw"), b("HL", S_[0:128]), A.subtract)
+    vs(b("HL", S_[128:256]), b("rawd"), 2048.0, A.add)
+    send(b("HL"), [(1, "la1", "a1"), (2, "la2", "a2")], NE)
+    send(b("HL"), [(4, "la4", "a4"), (3, "la3", "a3")], NE)
+    send(b("HL"), [(6, "la6", "a6")], NE)
+    for d in DEL:
+        arrives("la%d" % d, "a%d" % d, NE)
+    for t in NEXT:
+        for d in NEXT[t]:
+            arrives("lb%d%d" % (t, d), "b%d%d" % (t, d), NE)
+
+    def expand(n, src):
+        dma(bp(n, S_[0:128:16], S_[:]), b(src, S_[0:128]))
+        dma(bp(n, S_[1:128:16], S_[:]), b(src, S_[128:256]))
+    expand("tab0", "HL")
+    vs(b("KSc", S_[0:143]), b("IF", S_[0:143]), col["g15"], A.is_equal, col["is"], A.mult)
+    for d in (1, 2):
+        ms(b("tab%d" % d), 0.0)
+    expand("tab1", "la1")
+    expand("tab2", "la2")
+
+    def eye(n, c):
+        vs(b(n), b("IF", S_[0:128]), col["p"], A.is_equal, c, A.mult)
+
+    def blk(n, c):
+        vs(b(n), b("JG", S_[0:128]), col["g"], A.is_equal, c, A.mult)
+
+    def b8(n, c):
+        vs(b(n), b("IF", S_[0:8]), col["g"], A.is_equal, c, A.mult)
+    blk("Blk", 1.0)
+    vs(b("km"), b("IF", S_[0:16]), col["q"], A.is_equal)
+    vs(col["w"], col["po"], -2.0, A.mult, 1.0, A.add)
+    vs(col["po2"], col["po"], 2048.0, A.mult)
+    eye("I", 1.0)
+    for n, o, c in (("nI", "I", -1.0), ("I16", "I", 16.0), ("I256", "I", 256.0), ("I32", "I", 1.0), ("Iw", "I", col["w"]), ("Blk32", "Blk", 1.0),
+                    ("B4096", "Blk", 4096.0), ("BlkC", "Blk", col["is"])):
+        act(b(n), b(o), F.Copy, scale=c)
+    for n, c in (("Blk8", 1.0), ("Blk8c", col["is"]), ("B8h", 0.5), ("B8nh", -0.5)):
+        b8(n, c)
+
+    def hl_v(t):
+        act(b("vR"), b("vG%d" % t), bias=2048.0)
+        act(b("vW"), b("vR"), scale=col["w"])
+        act(b("vU"), b("vG%d" % t), bias=col["po2"], scale=col["po"])
+        vt(b("vHL%d" % t), b("vU"), b("vW"), A.add)
+
+    def vals(t):
+        iota(b("VV"), [[8, 256], [0, 16]], t, 0)
+
+    def wrap(bank, src, lo, hi):
+        bk = b(bank, S_[lo // 32:hi // 32])
+        for q in range(16):
+            mm(bk, b("KSc", S_[15 - q:143 - q]), b(src, S_[16 * lo + q:16 * hi:16]), q == 0, q == 15)
+
+    def unwrap(bank, out, lo, hi):
+        vs(b(out, S_[lo:hi]), b(bank, S_[lo // 32:hi // 32]), -2048.0, A.add)
+
+    def gath(e, out, w, o):
+        if e == "s":
+            act(out, ind(w, o))
+        else:
+            vc(out, ind(w, o))
+
+    def c1(s, h, e):
+        gath(e, b("T1", S_[1024 * h:1024 * h + 1024]), b("tab%d" % s, S_[:]), b("off0", S_[64 * h:64 * h + 64]))
+
+    def c2(u, h, e):
+        gath(e, b("DT", S_[1024 * h:1024 * h + 1024]), b("tab%d" % u, S_[:]), b("off1", S_[64 * h:64 * h + 64]))
+
+    def gather_d(h, e):
+        gath(e, b("dR", S_[2048 * h:2048 * h + 2048]), b("DT", S_[:]), b("a16", S_[128 * h:128 * h + 128]))
+
+    def gather_x(h):
+        gath("s", b("xk", S_[2048 * h:2048 * h + 2048]), b("X", S_[:]), b("a16", S_[128 * h:128 * h + 128]))
+
+    def sk_piece(t, j):
+        w = b("O", S_[0:2048]) if t else b("holI", S_[:])
+        vt(b("sk", S_[512 * j:512 * j + 512]), ind(w, b("a16", S_[32 * j:32 * j + 32])), b("VV", S_[512 * j:512 * j + 512]), A.is_equal)
+
+    def xv_mm(t):
+        for k in (0, 1):
+            mm(b("k0", S_[k::2]), b("I"), b("X", S_[t:2048:8]), True, True)
+
+    def min_v(p):
+        vt(b("mR", S_[512 * p:512 * p + 512]), b("xk", S_[p::8]), b("k0"), A.min)
+
+    def min_s(t, p):
+        bk = "k1" if p % 2 else "k2"
+        mm(b(bk), b("I"), b("xk", S_[p::8]), True, False)
+        for kk in (0, 1):
+            mm(b(bk, full, S_[kk::2]), b("nI"), b("X", S_[t:2048:8]), False, kk)
+        act(b("mR", S_[512 * p:512 * p + 512]), b(bk), F.Abs)
+
+    def m_mm(t, p):
+        for k in (p, p + 8):
+            for h in (0, 1):
+                l = b("mR", S_[512 * p + 256 * h + k // 8:512 * p + 256 * h + 256:2])
+                for o in ((k, k + 16) if k < 8 else (k,)):
+                    out = b("k5", S_[8 * h:8 * h + 8], o)
+                    if p < NV["min"]:
+                        mm(out, l, b("Blk8"), True, True)
+                    else:
+                        mm(out, b("xk", S_[2048 * h + k:2048 * h + 2048:16]), b("B8h"), True, False)
+                        mm(out, b("X", S_[1024 * h + t:1024 * h + 1024:8]), b("B8h"), False, False)
+                        mm(out, l, b("B8nh"), False, True)
+
+    def spread_max(src, least, mid=None):
+        mm(bp("k1", S_[0:16], S_[0:4]), b(src, S_[15::16]), b("I32"), True, True)
+        vs(bp("mx16", S_[0:16], S_[:]), bp("k1", S_[0:16], S_[0:4], full), least, A.max)
+        if mid:
+            mid()
+        for h in (0, 1):
+            mm(b("k2", S_[4 * h:4 * h + 4]), bp("E1", S_[0:16], S_[128 * h:128 * h + 128]), bp("mx16", S_[0:16], S_[:]), True, True)
+
+    vc(b("a16"), b("holI", S_[0:2048:8]))
+    wrap("k3", "tab0", 0, 128)
+    gather_x(0)
+    unwrap("k3", "off0", 0, 128)
+    for t in range(RO):
+        iota(b("vG%d" % t), [[8, 256]], t, 0)
+    vals(0)
+    iota(b("JM3"), [[0, 16], [1, 16]], 0, 0)
+    iota(b("k15"), [[0, 16], [-1, 16]], 15, 0)
+    for n, c in (("B8s", 1.0 / 16), ("B816", 16.0), ("B8n32", -32.0)):
+        b8(n, c)
+    vs(b("rst"), b("JM"), 0.0, A.is_gt)
+    vs(b("maskW"), b("JM"), col["q"], A.is_equal)
+    vs(b("kc"), b("JM"), -1.0, A.mult, 31.0, A.add)
+    vs(b("E1"), b("JG"), col["p"], A.is_equal)
+    vs(b("dumG"), b("IF"), 2048.0, A.add)
+    hl_v(0)
+    for j in range(2):
+        vc(b("O", S_[512 * j:512 * j + 512]), b("holI", S_[512 * j:512 * j + 512]))
+    c1(1, 0, "s")
+    c1(1, 1, "v")
+    gather_x(1)
+    for h in (0, 1):
+        wrap("k3", "T1", 64 * h, 64 * h + 64)
+    xv_mm(0)
+    sk_piece(0, 0)
+    for h in (0, 1):
+        unwrap("k3", "off1", 64 * h, 64 * h + 64)
+    c2(2, 0, "v")
+    c2(2, 1, "v")
+    gather_d(0, "s")
+    gather_d(1, "v")
+    vt(b("aD"), b("holI", S_[0:2048:8]), b("dumG"), A.subtract)
+    for j in range(2, 4):
+        fills.append(lambda j=j: vc(b("O", S_[512 * j:512 * j + 512]), b("holI", S_[512 * j:512 * j + 512])))
+    for d in (4, 3, 6):
+        dma(b("tab%d" % d), b("tab0"))
+        expand("tab%d" % d, "la%d" % d)
+
+    for t in range(RO):
+        if t:
+            gather_x(0)
+            gather_x(1)
+            gather_d(1, "v")
+            vt(b("oc"), b("O", S_[t - 1:2048:8]), b("ns"), A.mult)
+            vt(b("O", S_[t - 1:2048:8]), b("oc"), b("sb"), A.add)
+            gather_d(0, "s")
+            xv_mm(t)
+            vs(b("Z"), b("cnp"), 9.0, A.add)
+            sk_piece(t, 0)
+            vt(b("aD"), b("O", S_[t:2048:8]), b("dumG"), A.subtract)
+        fills[0:0] = [lambda j=j, t=t: sk_piece(t, j) for j in range(1, 8)]
+        for p in range(NV["min"]):
+            min_v(p)
+        for p in range(NV["min"], 8):
+            min_s(t, p)
+        if t == 0:
+            for k in range(16):
+                act(b("EK", S_[128 * k:128 * k + 128]), b("Blk"), F.Copy, scale=b("km", S_[k:k + 1]))
+
+        def c_mm(h):
+            for k in range(16):
+                mm(b("k4", S_[8 * h:8 * h + 8], k), b("dR", S_[2048 * h + k:2048 * h + 2048:16]), b("Blk8c"), True, True)
+        c_mm(1)
+        for p in range(8):
+            if p == 5:
+                c_mm(0)
+            m_mm(t, p)
+        act(b("md"), b("k5", full, S_[0:24]))
+        c4 = b("k4", full, S_[0:16])
+        vc(b("cd", full, S_[0:16]), c4)
+        vc(b("cd", full, S_[16:24]), b("k4", full, S_[0:8]))
+        if t == 0:
+            vs(b("dumW"), b("IF", S_[0:16]), 16.0, A.mult, col["q"], A.add)
+            fills.append(lambda: vs(b("dumW"), b("dumW"), 2048.0, A.add))
+            fills.append(lambda: vs(b("tri"), b("JM3"), col["q"], A.is_gt))
+            for h in (0, 8):
+                ms(b("fm", full, S_[0:NV["far"]]), 16.0)
+                ms(b("fm", full, S_[NV["far"]:8]), 0.0)
+                break
+            vt(b("BlkV"), b("Blk"), b("fm"), A.mult)
+            ms(b("zer"), 0.0)
+            ms(b("o16"), 1.0 / 16)
+            ms(b("Z"), 9.0)
+            ms(b("O", S_[2048:2304]), 0.0)
+        else:
+            fills.append(lambda t=t: hl_v(t))
+        pool = b("k6", full, S_[0:16])
+        mm(pool, b("I"), b("k15"), True, False)
+        mm(pool, b("I16"), b("md", full, S_[0:16]), False, False)
+        for s in range(1, 9):
+            eq = b("EQ", S_[16 * s - 16:16 * s], full)
+            vt(eq, b("cd", full, S_[s:s + 16]), c4, A.is_equal)
+            if s < 8:
+                j = s - 1
+                bank = "k1" if j // 2 % 2 == 0 else "k2"
+                reg = b(bank, full, S_[16 * (j % 2):16 * (j % 2) + 16])
+                mm(reg, b("I256"), eq, True, False)
+                mm(reg, b("I"), b("md", full, S_[0:16]), False, True)
+                if j % 2 or s == 7:
+                    w = 32 if j % 2 else 16
+                    act(b("PB", S_[16 * (j // 2):16 * (j // 2) + 16], S_[0:w]), b(bank, full, S_[0:w]), F.Relu, bias=-256.0)
+        act(b("cS"), c4)
+        for s in range(1, 9):
+            eq = b("EQ", S_[16 * s - 16:16 * s], full)
+            vt(b("PA", S_[16 * s - 16:16 * s], full), eq, b("k5", full, S_[s:s + 16]), A.mult)
+            if s < 8:
+                j = s - 1
+                z, o = S_[16 * (j // 2):16 * (j // 2) + 16], 16 * (j % 2)
+                mm(b("k6", full, S_[s:16]), b("I16"), b("PB", z, S_[o:o + 16 - s]), False, False)
+                mm(b("k6", full, S_[0:s]), b("I16"), b("PB", z, S_[o + 16 - s:o + 16]), False, False)
+            mm(pool, b("I16"), b("PA", S_[16 * s - 16:16 * s], full), False, s == 8)
+        fill(1)
+        for h in (0, 1):
+            mm(b("k3", S_[4 * h:4 * h + 4]), b("cS", S_[128 * h:128 * h + 128]), b("I32"), True, True)
+        act(b("cK"), b("k3", S_[0:8]), bias=-2048.0)
+        vc(b("keyS"), pool)
+        scan(b("mxS"), b("rst"), b("keyS"), A.mult, A.max)
+        for h in (0, 1):
+            mm(b("k3", S_[8 + 4 * h:12 + 4 * h]), b("keyS", S_[128 * h:128 * h + 128]), b("I32"), True, True)
+        act(b("keyK"), b("k3", S_[8:16]))
+        fl = b("k7", S_[0:256])
+
+        def far_const():
+            mm(fl, b("I"), b("kc"), True, False)
+            for p in range(NV["far"]):
+                for k in (p, p + 8):
+                    for h in (0, 1):
+                        mm(b("k7", S_[128 * h + k:128 * h + 128:16]), b("xk", S_[2048 * h + k:2048 * h + 2048:16]), b("B816"), False, False)
+        fill(1)
+        spread_max("mxS", 0.0, lambda: fill(1))
+        vt(b("oh"), b("keyK"), b("k2", S_[0:8]), A.is_equal)
+        vt(b("ohc"), b("oh"), b("cK"), A.mult)
+        bG = b("k0", S_[0:256])
+        mm(bG, b("Blk32"), b("ohc"), True, True)
+        far_const()
+        fill(1)
+        vt(b("mine"), b("cK"), bG, A.is_equal)
+        vs(b("w1"), b("mine"), 2.0, A.mult, -1.0, A.add)
+        act(b("w16"), b("mine"), scale=32.0, bias=-16.0)
+        vt(b("bw"), bG, b("maskW"), A.mult)
+        scan(b("bws"), b("rst"), b("bw"), A.mult, A.add)
+        vc(b("bo"), b("bws", S_[15::16]))
+        dps = b("k5", S_[0:8])
+        first = [True]
+        nv, ns_ = [0], [0]
+
+        def vbank():
+            nv[0] += 1
+            return "k1" if nv[0] % 2 else "k2"
+
+        def sbank():
+            ns_[0] += 1
+            return "k4" if ns_[0] % 2 else "k3"
+
+        def win_feed(p):
+            vec = p < NV["win"]
+            bk = vbank() if vec else sbank()
+            if not vec:
+                mm(b(bk), b("I"), b("xk", S_[p::8]), True, False)
+            for kk in (0, 1):
+                k = p + 8 * kk
+                mm(b(bk, full, S_[kk::2]), b("EK", S_[128 * k:128 * k + 128]), b("w1" if vec else "w16"), vec, vec or kk)
+            o = b("pR", S_[512 * p:512 * p + 512])
+            if vec:
+                vt(o, b("xk", S_[p::8]), b(bk), A.mult)
+            else:
+                act(o, b(bk), F.Abs)
+
+        def win_acc(p, last):
+            for kk in (0, 1):
+                mm(dps, b("I"), b("pR", S_[512 * p + kk:512 * p + 512:2]), first[0], last and kk)
+                first[0] = False
+
+        def mix(nv_):
+            vps, sps = list(range(nv_)), list(range(nv_, 8))
+            out = []
+            for j in range(8):
+                out += vps[j:j + 1] + sps[j:j + 1]
+            return out
+        order = mix(NV["win"])
+        for p in order[:2]:
+            win_feed(p)
+        fill(99)
+        for p in order[2:4]:
+            win_feed(p)
+        act(b("xb"), ind(b("X", S_[:]), b("bo")))
+        hd = b("k0", S_[256:512])
+        act(b("hR"), bG, bias=2048.0)
+        act(b("hU"), bG, bias=col["po2"], scale=col["po"])
+        if t == 1:
+            for d in (3, 6):
+                act(b("tab%d" % d, S_[0:2048:8]), b("lb0%d" % d))
+        for h in (0, 1):
+            mm(b("k6", S_[4 * h:4 * h + 4]), b("mine", S_[128 * h:128 * h + 128]), b("I"), True, True)
+            for k in range(16):
+                mm(b("k6", S_[8 + 4 * h:12 + 4 * h], S_[k::16]), b("sk", S_[2048 * h + k:2048 * h + 2048:16]), b("B8s"), True, True)
+        act(b("st"), b("k6", S_[8:16]))
+        for j, p in enumerate(order):
+            if j == 2:
+                mm(hd, b("Iw"), b("hR"), True, False)
+                mm(hd, b("nI"), b("vHL%d" % t), False, True)
+            win_acc(p, j == 7)
+            if j + 4 < 8:
+                win_feed(order[j + 4])
+        vt(b("el"), b("st"), b("k6", S_[0:8]), A.is_gt)
+        for kk in (0, 1):
+            mm(b("k6", full, S_[kk::2]), b("I"), b("xb"), True, True)
+        for h in (0, 1):
+            mm(b("k7", S_[128 * h:128 * h + 128]), b("xb", S_[128 * h:128 * h + 128]), b("BlkV"), False, False)
+        forder = mix(NV["far"])
+
+        def far_feed(p):
+            o = b("mR", S_[512 * p:512 * p + 512])
+            if p < NV["far"]:
+                vt(o, b("xk", S_[p::8]), b("k6"), A.min)
+            else:
+                bk = sbank()
+                mm(b(bk), b("I"), b("xk", S_[p::8]), True, False)
+                for kk in (0, 1):
+                    mm(b(bk, full, S_[kk::2]), b("nI"), b("xb"), False, kk)
+                act(o, b(bk), F.Abs)
+
+        def far_acc(p, last):
+            for k in (p, p + 8):
+                for h in (0, 1):
+                    mm(b("k7", S_[128 * h + k:128 * h + 128:16]), b("mR", S_[512 * p + 256 * h + k // 8:512 * p + 256 * h + 256:2]),
+                       b("B8n32" if p < NV["far"] else "B816"), False, last and k > 7 and h)
+        vs(b("gt"), dps, 32.0 * (8 - NV["win"]), A.is_gt)
+        for p in forder[:2]:
+            far_feed(p)
+        for h in (0, 1):
+            mm(b("k1", S_[4 * h:4 * h + 4]), b("gt", S_[128 * h:128 * h + 128]), b("Blk"), True, True)
+        mm(b("k2", S_[0:8]), b("Blk"), b("gt"), True, True)
+        far_feed(forder[2])
+        vt(hd, b("hU"), hd, A.add)
+        vs(b("winG"), b("k2", S_[0:8]), b("Z"), A.is_ge)
+        vt(hd, b("winG"), hd, A.mult)
+        CN = "CN%d" % t
+        vt(b(CN), b("vHL%d" % t), hd, A.add)
+        if t in NEXT:
+            ds = NEXT[t]
+            for j in range(0, len(ds), 2):
+                send(b(CN), [(d, "lb%d%d" % (t, d), "b%d%d" % (t, d)) for d in ds[j:j + 2]], NE)
+            vals(t + 1)
+        vc(b("tab0", S_[t:2048:8]), b(CN))
+        far_feed(forder[3])
+        for p in forder[:3]:
+            far_acc(p, False)
+        nxt = t < RO - 1
+        goal = b("k5", full, S_[0:16])
+        mm(goal, b("I32"), b("dumG"), True, False)
+        if nxt:
+            wrap("k2", "tab0", 0, 128)
+        for p in forder[4:6]:
+            far_feed(p)
+        vs(b("k1", S_[0:8]), b("k1", S_[0:8]), b("Z"), A.is_ge)
+        vt(b("elw"), b("el"), b("k1", S_[0:8]), A.mult)
+        for p in forder[3:5]:
+            far_acc(p, False)
+        for j in (6, 7):
+            far_feed(forder[j])
+        for j in (5, 6, 7):
+            far_acc(forder[j], j == 7)
+        vt(b("FK"), b("elw"), fl, A.mult)
+        scan(b("fS"), b("rst"), b("FK"), A.mult, A.max)
+        for h in (0, 1):
+            mm(b("k4", S_[4 * h:4 * h + 4]), b("FK", S_[128 * h:128 * h + 128]), b("I32"), True, True)
+        act(b("FKk"), b("k4", S_[0:8]))
+        if nxt:
+            unwrap("k2", "off0", 0, 128)
+            op("v", lambda: v.tensor_reduce(ap(b("cnw")), ap(b("winG")), AxisListType.X, A.add), [b("winG")], [b("cnw")])
+        spread_max("fS", 1.0)
+        if nxt:
+            mm(b("k3", 15, S_[31:32]), b("o16"), b("cnw"), True, True)
+            vc(b("cni"), b("k3", 15, S_[31:32]))
+            vs(b("cnp"), b("cni"), 1, A.bitwise_and)
+            s_, u_ = NEXT[t][0] if t == 0 else 3, NEXT[t][1] if t == 0 else 6
+            for d in (s_, u_):
+                act(b("tab%d" % d, S_[t:2048:8]), b("lb%d%d" % (t, d)))
+        vt(b("soh"), b("FKk"), b("k2", S_[0:8]), A.is_equal)
+        vt(b("ga"), b("soh"), b("aD"), A.mult)
+        mm(goal, b("Blk32"), b("ga"), False, True)
+        vt(b("ca"), b("soh"), b("cK"), A.mult)
+        csG = b("k6", S_[0:8])
+        mm(csG, b("Blk32"), b("ca"), True, True)
+        if nxt:
+            for h in (0, 1):
+                c1(s_, h, "s")
+        vt(b("gw"), goal, b("maskW"), A.mult)
+        scan(b("gws"), b("rst"), b("gw"), A.mult, A.add)
+        vc(b("gSu"), goal)
+        vc(b("go"), b("gws", S_[15::16]))
+        act(b("OG"), ind(b("O", S_[:]), b("go")))
+        act(b("ns"), b("soh"), scale=-1.0, bias=1.0)
+        dup = b("k4", full, S_[0:16])
+        mm(dup, b("I"), b("zer"), True, False)
+        for c in range(16):
+            vs(b("E3", c, S_[0:256 - 16 * c]), b("gSu", S_[16 * c:256]), b("gws", S_[16 * c + 15:16 * c + 16]), A.is_equal)
+            if c < 15:
+                mm(b("k4", S_[c + 1:16], S_[0:16]), b("B4096"), b("E3", c, S_[16:256 - 16 * c]), False, False)
+            if nxt and c in (1, 6):
+                h = c // 6
+                wrap("k3", "T1", 64 * h, 64 * h + 64)
+            if nxt and c in (8, 13):
+                h = c // 13
+                unwrap("k3", "off1", 64 * h, 64 * h + 64)
+                c2(u_, h, "s")
+        vt(b("E3", full, S_[0:16]), b("E3", full, S_[0:16]), b("tri"), A.mult)
+        mm(dup, b("B4096"), b("E3", full, S_[0:16]), False, True)
+        vt(b("eqv"), b("OG"), b("vG%d" % t), A.is_equal)
+        vt(b("dd"), csG, b("OG"), A.subtract)
+        vt(b("tt"), b("eqv"), b("dd"), A.mult)
+        vt(b("dw"), dup, b("maskW"), A.mult)
+        scan(b("dws"), b("rst"), b("dw"), A.mult, A.add)
+        vt(b("t1"), b("dws", S_[15::16]), b("dumW"), A.min)
+        vt(b("sb"), b("soh"), bG, A.mult)
+        vt(b("t2"), b("t1"), b("gws", S_[15::16]), A.max)
+        vc(b("so"), b("t2"))
+        vt(ind(b("O", S_[:]), b("so")), b("OG"), b("tt"), A.add)
+        if not nxt:
+            break
+        vc(b("a16"), b("O", S_[t + 1:2048:8]))
+    t = RO - 1
+    vt(b("oc"), b("O", S_[t:2048:8]), b("ns"), A.mult)
+    vt(b("O", S_[t:2048:8]), b("oc"), b("sb"), A.add)
+    for j, bk in enumerate(("k1", "k2", "k3", "k4")):
+        mm(b(bk), b("BlkC"), b("tab0", S_[512 * j:512 * j + 512]), True, True)
+        act(b("ycS", S_[512 * j:512 * j + 512]), b(bk), bias=-2048.0)
+    dma(("yo", S_[:]), b("O", S_[0:2048]))
+    dma(("yc", S_[:]), bp("ycS", S_[0:128:16], S_[:]))
+    for s, n in cnt.items():
+        g.wait_ge(T.sem[s], n)
+    g.wait_ge(T.sem.ls, nls[0])

@@ -5,7 +5,8 @@ from concourse.bass import DstId, RemoteDMATransfer
 V, D, L, RO, N = 2048, 8, 256, 3, 8
 DEL = (1, 2, 4, 3, 6)
 NEXT = {0: (2, 4, 3, 6), 1: (3, 6)}
-NV = {"min": 7, "win": 5, "far": 4}
+NV = {"min": 8, "win": 5, "far": 6, "d": 128, "sk": 2, "sk2": 0, "c0": 5, "c1": 0}
+NA = 1
 S_ = np.s_
 
 _bf, _f, _i, _u = "bfloat16", "float32", "int32", "uint16"
@@ -14,20 +15,20 @@ _shapes = {
     "HL": ([256], _bf), "VV": ([4096], _f), "xk": ([4096], _bf), "sk": ([4096], _bf), "dR": ([4096], _bf),
     "mR": ([4096], _bf), "pR": ([4096], _bf), "T1": ([2048], _bf), "DT": ([2048], _bf), "EK": ([2048], _bf),
     "E3": ([16, 272], _bf), "ycS": ([2048], _f),
-    "EQ": ([128, 16], _bf), "PA": ([128, 16], _bf), "PB": ([64, 32], _bf),
+    "EQ": ([128, 16], _bf), "PA": ([128, 16], _bf), "PB": ([80, 32], _bf),
     "off0": ([128], _u), "off1": ([128], _u), "a16": ([256], _u), "bo": ([16], _u), "go": ([16], _u), "so": ([16], _u),
     "gSu": ([256], _u), "aD": ([256], _f), "cd": ([16, 24], _f), "md": ([16, 24], _bf), "cS": ([256], _f),
-    "keyS": ([256], _f), "mxS": ([256], _f), "keyK": ([256], _f), "mx16": ([128], _f), "oh": ([256], _f), "ohc": ([256], _f),
+    "bU": ([256], _f), "keyS": ([256], _f), "mxS": ([256], _f), "keyK": ([256], _f), "mx16": ([128], _f), "ohc": ([256], _f),
     "cK": ([256], _f), "mine": ([256], _bf), "w1": ([256], _bf), "w16": ([256], _bf), "bw": ([256], _f), "bws": ([256], _f),
-    "xb": ([256], _bf), "gt": ([256], _bf), "winG": ([256], _f), "st": ([256], _bf), "el": ([256], _f), "elw": ([256], _f),
-    "FK": ([256], _f), "FKk": ([256], _f), "fS": ([256], _f), "soh": ([256], _f), "ga": ([256], _f), "ca": ([256], _f), "ns": ([256], _f),
+    "xb": ([256], _bf), "gt": ([256], _bf), "wl": ([256], _bf), "winG": ([256], _f), "st": ([256], _bf), "el": ([256], _f), "elw": ([256], _f),
+    "FK": ([256], _f), "FKk": ([256], _f), "fS": ([256], _f), "ga": ([256], _f), "ca": ([256], _f), "ns": ([256], _f),
     "sb": ([256], _f), "gw": ([256], _f), "gws": ([256], _f), "OG": ([256], _f), "dw": ([256], _f), "dws": ([256], _f),
     "t1": ([16], _f), "t2": ([16], _f), "eqv": ([256], _f), "dd": ([256], _f), "tt": ([256], _f), "oc": ([256], _f),
     "hR": ([256], _bf), "hU": ([256], _f), "vR": ([256], _bf), "vW": ([256], _bf), "vU": ([256], _f),
     "cnw": ([1], _f), "cni": ([1], _i), "cnp": ([1], _i), "Z": ([1], _f),
     "IF": ([256], _f), "JG": ([256], _f), "JM": ([256], _f), "JM3": ([16, 16], _f), "pi": ([1], _i), "qi": ([1], _i),
     "cols": ([16], _f), "I": ([128], _bf), "I16": ([128], _bf), "I256": ([128], _bf), "nI": ([128], _bf), "Iw": ([128], _bf),
-    "I32": ([128], _f), "Blk": ([128], _bf), "Blk32": ([128], _f), "BlkC": ([128], _bf), "B4096": ([128], _bf), "BlkV": ([128], _bf),
+    "I32": ([128], _f), "Ip32": ([128], _f), "Blk": ([128], _bf), "Blk32": ([128], _f), "BlkC": ([128], _bf), "B4096": ([128], _bf), "BlkV": ([128], _bf),
     "fm": ([16, 8], _bf), "Blk8": ([8], _bf), "Blk8c": ([8], _bf), "B8s": ([8], _bf), "B816": ([8], _bf), "B8n32": ([8], _bf),
     "B8h": ([8], _bf), "B8nh": ([8], _bf), "KSc": ([144], _bf),
     "km": ([16], _f), "maskW": ([256], _f), "rst": ([256], _f), "tri": ([16, 16], _bf), "E1": ([256], _f), "k15": ([16, 16], _bf),
@@ -35,7 +36,7 @@ _shapes = {
 }
 SCRATCH = {n: ("sbuf", [128] + s, d) for n, (s, d) in _shapes.items()}
 PACK = {n: 256 * j for j, n in enumerate((
-    "aD cS keyS mxS keyK oh ohc cK bw bws el elw winG FK FKk fS soh ga ca ns sb gw gws OG dw dws eqv dd tt oc hU vU").split())}
+    "aD cS keyS mxS keyK ohc cK bw bws el elw winG FK FKk fS ga ca bU sb gw gws OG dw dws eqv tt hU vU").split())}
 SHAPE = dict(SCRATCH)
 for _n in PACK:
     del SCRATCH[_n]
@@ -234,28 +235,6 @@ def rank_program(g, core, T, topo):
     vs(col["is"], col["q"], 2.0, A.is_lt)
     vc(col["po"], b("cni"))
     vs(col["g15"], col["g15"], 15.0, A.add)
-    ms(b("tab0"), 0.0)
-    vs(b("HL", S_[0:128]), b("raw"), 2048.0, A.add)
-    vt(b("rawd"), b("raw"), b("HL", S_[0:128]), A.subtract)
-    vs(b("HL", S_[128:256]), b("rawd"), 2048.0, A.add)
-    send(b("HL"), [(1, "la1", "a1"), (2, "la2", "a2")], NE)
-    send(b("HL"), [(4, "la4", "a4"), (3, "la3", "a3")], NE)
-    send(b("HL"), [(6, "la6", "a6")], NE)
-    for d in DEL:
-        arrives("la%d" % d, "a%d" % d, NE)
-    for t in NEXT:
-        for d in NEXT[t]:
-            arrives("lb%d%d" % (t, d), "b%d%d" % (t, d), NE)
-
-    def expand(n, src):
-        dma(bp(n, S_[0:128:16], S_[:]), b(src, S_[0:128]))
-        dma(bp(n, S_[1:128:16], S_[:]), b(src, S_[128:256]))
-    expand("tab0", "HL")
-    vs(b("KSc", S_[0:143]), b("IF", S_[0:143]), col["g15"], A.is_equal, col["is"], A.mult)
-    for d in (1, 2):
-        ms(b("tab%d" % d), 0.0)
-    expand("tab1", "la1")
-    expand("tab2", "la2")
 
     def eye(n, c):
         vs(b(n), b("IF", S_[0:128]), col["p"], A.is_equal, c, A.mult)
@@ -267,10 +246,42 @@ def rank_program(g, core, T, topo):
         vs(b(n), b("IF", S_[0:8]), col["g"], A.is_equal, c, A.mult)
     blk("Blk", 1.0)
     vs(b("km"), b("IF", S_[0:16]), col["q"], A.is_equal)
+    for k in range(16):
+        act(b("EK", S_[128 * k:128 * k + 128]), b("Blk"), F.Copy, scale=b("km", S_[k:k + 1]))
+    eye("I", 1.0)
+    vs(b("HL", S_[0:128]), b("raw"), 2048.0, A.add)
+    vt(b("rawd"), b("raw"), b("HL", S_[0:128]), A.subtract)
+    vs(b("HL", S_[128:256]), b("rawd"), 2048.0, A.add)
+    ms(b("tab0"), 0.0)
+    send(b("HL"), [(1, "la1", "a1"), (2, "la2", "a2")], NE)
+    send(b("HL"), [(4, "la4", "a4"), (3, "la3", "a3")], NE)
+    send(b("HL"), [(6, "la6", "a6")], NE)
+    for d in DEL:
+        arrives("la%d" % d, "a%d" % d, NE)
+    for t in NEXT:
+        for d in NEXT[t]:
+            arrives("lb%d%d" % (t, d), "b%d%d" % (t, d), NE)
+
+    def expand(n, src):
+        o = [bp(n, S_[h:128:16], S_[:]) for h in (0, 1)]
+        waits("y", need("y", [b(src)], [o[0]]))
+        for h in (0, 1):
+            s = "d%d" % ndma[0]
+            ndma[0] += 1
+            cnt[s] = 16
+            g.sync.dma_start(ap(o[h]), ap(b(src, S_[128 * h:128 * h + 128]))).then_inc(T.sem[s], 16)
+            hist[(s, 16)] = dict(clk["y"])
+            note(R, b(src), s, 16)
+            note(W, o[h], s, 16)
+    expand("tab0", "HL")
+    vs(b("KSc", S_[0:143]), b("IF", S_[0:143]), col["g15"], A.is_equal, col["is"], A.mult)
+    for d in (1, 2):
+        ms(b("tab%d" % d), 0.0)
+    expand("tab1", "la1")
+    expand("tab2", "la2")
     vs(col["w"], col["po"], -2.0, A.mult, 1.0, A.add)
     vs(col["po2"], col["po"], 2048.0, A.mult)
-    eye("I", 1.0)
-    for n, o, c in (("nI", "I", -1.0), ("I16", "I", 16.0), ("I256", "I", 256.0), ("I32", "I", 1.0), ("Iw", "I", col["w"]), ("Blk32", "Blk", 1.0),
+    for n, o, c in (("nI", "I", -1.0), ("I16", "I", 16.0), ("I256", "I", 256.0), ("I32", "I", 1.0), ("Iw", "I", col["w"]), ("Ip32", "I", col["po"]), ("Blk32", "Blk", 1.0),
                     ("B4096", "Blk", 4096.0), ("BlkC", "Blk", col["is"])):
         act(b(n), b(o), F.Copy, scale=c)
     for n, c in (("Blk8", 1.0), ("Blk8c", col["is"]), ("B8h", 0.5), ("B8nh", -0.5)):
@@ -278,9 +289,10 @@ def rank_program(g, core, T, topo):
 
     def hl_v(t):
         act(b("vR"), b("vG%d" % t), bias=2048.0)
-        act(b("vW"), b("vR"), scale=col["w"])
-        act(b("vU"), b("vG%d" % t), bias=col["po2"], scale=col["po"])
-        vt(b("vHL%d" % t), b("vU"), b("vW"), A.add)
+        act(b("vU"), b("vG%d" % t), bias=2048.0)
+        mm(b("k4", S_[0:8]), b("Iw"), b("vR"), True, False)
+        mm(b("k4", S_[0:8]), b("Ip32"), b("vU"), False, True)
+        act(b("vHL%d" % t), b("k4", S_[0:8]))
 
     def vals(t):
         iota(b("VV"), [[8, 256], [0, 16]], t, 0)
@@ -305,8 +317,8 @@ def rank_program(g, core, T, topo):
     def c2(u, h, e):
         gath(e, b("DT", S_[1024 * h:1024 * h + 1024]), b("tab%d" % u, S_[:]), b("off1", S_[64 * h:64 * h + 64]))
 
-    def gather_d(h, e):
-        gath(e, b("dR", S_[2048 * h:2048 * h + 2048]), b("DT", S_[:]), b("a16", S_[128 * h:128 * h + 128]))
+    def gather_d(lo, hi, e):
+        gath(e, b("dR", S_[16 * lo:16 * hi]), b("DT", S_[:]), b("a16", S_[lo:hi]))
 
     def gather_x(h):
         gath("s", b("xk", S_[2048 * h:2048 * h + 2048]), b("X", S_[:]), b("a16", S_[128 * h:128 * h + 128]))
@@ -350,13 +362,28 @@ def rank_program(g, core, T, topo):
         for h in (0, 1):
             mm(b("k2", S_[4 * h:4 * h + 4]), bp("E1", S_[0:16], S_[128 * h:128 * h + 128]), bp("mx16", S_[0:16], S_[:]), True, True)
 
+    rest = b("k7", S_[256:512])
+
+    def sellers(t):
+        vt(rest, b("O", S_[t:2048:8]), rest, A.mult)
+        vt(b("O", S_[t:2048:8]), b("sb"), rest, A.add)
+
+    ms(b("fm", full, S_[0:NV["far"]]), 16.0)
+    ms(b("fm", full, S_[NV["far"]:8]), 0.0)
+    ms(b("zer"), 0.0)
+    ms(b("o16"), 1.0 / 16)
+    ms(b("Z"), 9.0)
+    ms(b("O", S_[2048:2304]), 0.0)
+    vs(b("dumW"), b("IF", S_[0:16]), 16.0, A.mult, col["q"], A.add)
+    vt(b("BlkV"), b("Blk"), b("fm"), A.mult)
+    vs(b("dumW"), b("dumW"), 2048.0, A.add)
     vc(b("a16"), b("holI", S_[0:2048:8]))
     wrap("k3", "tab0", 0, 128)
     gather_x(0)
     unwrap("k3", "off0", 0, 128)
+    vals(0)
     for t in range(RO):
         iota(b("vG%d" % t), [[8, 256]], t, 0)
-    vals(0)
     iota(b("JM3"), [[0, 16], [1, 16]], 0, 0)
     iota(b("k15"), [[0, 16], [-1, 16]], 15, 0)
     for n, c in (("B8s", 1.0 / 16), ("B816", 16.0), ("B8n32", -32.0)):
@@ -366,24 +393,22 @@ def rank_program(g, core, T, topo):
     vs(b("kc"), b("JM"), -1.0, A.mult, 31.0, A.add)
     vs(b("E1"), b("JG"), col["p"], A.is_equal)
     vs(b("dumG"), b("IF"), 2048.0, A.add)
-    hl_v(0)
-    for j in range(2):
-        vc(b("O", S_[512 * j:512 * j + 512]), b("holI", S_[512 * j:512 * j + 512]))
     c1(1, 0, "s")
     c1(1, 1, "v")
+    for j in range(3):
+        vc(b("O", S_[512 * j:512 * j + 512]), b("holI", S_[512 * j:512 * j + 512]))
     gather_x(1)
-    for h in (0, 1):
+    for h in (1, 0):
         wrap("k3", "T1", 64 * h, 64 * h + 64)
     xv_mm(0)
-    sk_piece(0, 0)
-    for h in (0, 1):
+    for h in (1, 0):
         unwrap("k3", "off1", 64 * h, 64 * h + 64)
-    c2(2, 0, "v")
-    c2(2, 1, "v")
-    gather_d(0, "s")
-    gather_d(1, "v")
+        c2(2, h, "v")
+    gather_d(0, 128, "s")
+    gather_d(128, 256, "v")
     vt(b("aD"), b("holI", S_[0:2048:8]), b("dumG"), A.subtract)
-    for j in range(2, 4):
+    fills.append(lambda: vs(b("tri"), b("JM3"), col["q"], A.is_gt))
+    for j in range(3, 4):
         fills.append(lambda j=j: vc(b("O", S_[512 * j:512 * j + 512]), b("holI", S_[512 * j:512 * j + 512])))
     for d in (4, 3, 6):
         dma(b("tab%d" % d), b("tab0"))
@@ -393,75 +418,69 @@ def rank_program(g, core, T, topo):
         if t:
             gather_x(0)
             gather_x(1)
-            gather_d(1, "v")
-            vt(b("oc"), b("O", S_[t - 1:2048:8]), b("ns"), A.mult)
-            vt(b("O", S_[t - 1:2048:8]), b("oc"), b("sb"), A.add)
-            gather_d(0, "s")
+            gather_d(NV["d"], 256, "v")
+            sellers(t - 1)
+            gather_d(0, NV["d"], "s")
             xv_mm(t)
             vs(b("Z"), b("cnp"), 9.0, A.add)
-            sk_piece(t, 0)
+            for j in range(NV["sk"]):
+                sk_piece(t, j)
             vt(b("aD"), b("O", S_[t:2048:8]), b("dumG"), A.subtract)
-        fills[0:0] = [lambda j=j, t=t: sk_piece(t, j) for j in range(1, 8)]
+        fills[0:0] = [lambda j=j, t=t: sk_piece(t, j) for j in range(NV["sk"] if t else 0, 8)]
         for p in range(NV["min"]):
             min_v(p)
+        if t:
+            fill(NV["sk2"])
         for p in range(NV["min"], 8):
             min_s(t, p)
-        if t == 0:
-            for k in range(16):
-                act(b("EK", S_[128 * k:128 * k + 128]), b("Blk"), F.Copy, scale=b("km", S_[k:k + 1]))
 
         def c_mm(h):
             for k in range(16):
                 mm(b("k4", S_[8 * h:8 * h + 8], k), b("dR", S_[2048 * h + k:2048 * h + 2048:16]), b("Blk8c"), True, True)
-        c_mm(1)
         for p in range(8):
-            if p == 5:
+            if p == NV["c0"]:
                 c_mm(0)
+            if p == NV["c1"]:
+                c_mm(1)
             m_mm(t, p)
         act(b("md"), b("k5", full, S_[0:24]))
         c4 = b("k4", full, S_[0:16])
         vc(b("cd", full, S_[0:16]), c4)
         vc(b("cd", full, S_[16:24]), b("k4", full, S_[0:8]))
-        if t == 0:
-            vs(b("dumW"), b("IF", S_[0:16]), 16.0, A.mult, col["q"], A.add)
-            fills.append(lambda: vs(b("dumW"), b("dumW"), 2048.0, A.add))
-            fills.append(lambda: vs(b("tri"), b("JM3"), col["q"], A.is_gt))
-            for h in (0, 8):
-                ms(b("fm", full, S_[0:NV["far"]]), 16.0)
-                ms(b("fm", full, S_[NV["far"]:8]), 0.0)
-                break
-            vt(b("BlkV"), b("Blk"), b("fm"), A.mult)
-            ms(b("zer"), 0.0)
-            ms(b("o16"), 1.0 / 16)
-            ms(b("Z"), 9.0)
-            ms(b("O", S_[2048:2304]), 0.0)
-        else:
-            fills.append(lambda t=t: hl_v(t))
         pool = b("k6", full, S_[0:16])
         mm(pool, b("I"), b("k15"), True, False)
         mm(pool, b("I16"), b("md", full, S_[0:16]), False, False)
+        back = [(1, s) for s in range(1, 9 - NA)] + [x for s in range(9 - NA, 9) for x in ((1, s), (0, s)) if x != (1, 8)]
         for s in range(1, 9):
             eq = b("EQ", S_[16 * s - 16:16 * s], full)
             vt(eq, b("cd", full, S_[s:s + 16]), c4, A.is_equal)
-            if s < 8:
-                j = s - 1
+            for j, (way, r) in enumerate(back):
+                if r != s:
+                    continue
                 bank = "k1" if j // 2 % 2 == 0 else "k2"
                 reg = b(bank, full, S_[16 * (j % 2):16 * (j % 2) + 16])
                 mm(reg, b("I256"), eq, True, False)
-                mm(reg, b("I"), b("md", full, S_[0:16]), False, True)
-                if j % 2 or s == 7:
-                    w = 32 if j % 2 else 16
-                    act(b("PB", S_[16 * (j // 2):16 * (j // 2) + 16], S_[0:w]), b(bank, full, S_[0:w]), F.Relu, bias=-256.0)
+                mm(reg, b("I"), b("md", full, S_[0:16] if way else S_[s:s + 16]), False, True)
+                if j % 2:
+                    act(b("PB", S_[8 * j - 8:8 * j + 8], full), b(bank, full, full), F.Relu, bias=-256.0)
         act(b("cS"), c4)
-        for s in range(1, 9):
-            eq = b("EQ", S_[16 * s - 16:16 * s], full)
-            vt(b("PA", S_[16 * s - 16:16 * s], full), eq, b("k5", full, S_[s:s + 16]), A.mult)
-            if s < 8:
-                j = s - 1
-                z, o = S_[16 * (j // 2):16 * (j // 2) + 16], 16 * (j % 2)
+
+        def pool_b(j):
+            way, s = back[j]
+            z, o = S_[16 * (j // 2):16 * (j // 2) + 16], 16 * (j % 2)
+            if way:
                 mm(b("k6", full, S_[s:16]), b("I16"), b("PB", z, S_[o:o + 16 - s]), False, False)
                 mm(b("k6", full, S_[0:s]), b("I16"), b("PB", z, S_[o + 16 - s:o + 16]), False, False)
-            mm(pool, b("I16"), b("PA", S_[16 * s - 16:16 * s], full), False, s == 8)
+            else:
+                mm(pool, b("I16"), b("PB", z, S_[o:o + 16]), False, j == len(back) - 1)
+        for s in range(1, 9 - NA):
+            eq = b("EQ", S_[16 * s - 16:16 * s], full)
+            vt(b("PA", S_[16 * s - 16:16 * s], full), eq, b("k5", full, S_[s:s + 16]), A.mult)
+            mm(pool, b("I16"), b("PA", S_[16 * s - 16:16 * s], full), False, False)
+            if s > 1:
+                pool_b(s - 2)
+        for j in range(7 - NA, len(back)):
+            pool_b(j)
         fill(1)
         for h in (0, 1):
             mm(b("k3", S_[4 * h:4 * h + 4]), b("cS", S_[128 * h:128 * h + 128]), b("I32"), True, True)
@@ -472,6 +491,10 @@ def rank_program(g, core, T, topo):
             mm(b("k3", S_[8 + 4 * h:12 + 4 * h]), b("keyS", S_[128 * h:128 * h + 128]), b("I32"), True, True)
         act(b("keyK"), b("k3", S_[8:16]))
         fl = b("k7", S_[0:256])
+        if t == 1:
+            for d in (3, 6):
+                act(b("tab%d" % d, S_[0:2048:8]), b("lb0%d" % d))
+        fl = b("k7", S_[0:256])
 
         def far_const():
             mm(fl, b("I"), b("kc"), True, False)
@@ -481,8 +504,14 @@ def rank_program(g, core, T, topo):
                         mm(b("k7", S_[128 * h + k:128 * h + 128:16]), b("xk", S_[2048 * h + k:2048 * h + 2048:16]), b("B816"), False, False)
         fill(1)
         spread_max("mxS", 0.0, lambda: fill(1))
-        vt(b("oh"), b("keyK"), b("k2", S_[0:8]), A.is_equal)
-        vt(b("ohc"), b("oh"), b("cK"), A.mult)
+        hl_v(t)
+
+        def stakes(h):
+            for k in range(16):
+                mm(b("k6", S_[8 + 4 * h:12 + 4 * h], S_[k::16]), b("sk", S_[2048 * h + k:2048 * h + 2048:16]), b("B8s"), True, True)
+        hot = b("k1", S_[8:16])
+        vt(hot, b("keyK"), b("k2", S_[0:8]), A.is_equal)
+        vt(b("ohc"), b("cK"), hot, A.mult)
         bG = b("k0", S_[0:256])
         mm(bG, b("Blk32"), b("ohc"), True, True)
         far_const()
@@ -540,14 +569,8 @@ def rank_program(g, core, T, topo):
         hd = b("k0", S_[256:512])
         act(b("hR"), bG, bias=2048.0)
         act(b("hU"), bG, bias=col["po2"], scale=col["po"])
-        if t == 1:
-            for d in (3, 6):
-                act(b("tab%d" % d, S_[0:2048:8]), b("lb0%d" % d))
-        for h in (0, 1):
-            mm(b("k6", S_[4 * h:4 * h + 4]), b("mine", S_[128 * h:128 * h + 128]), b("I"), True, True)
-            for k in range(16):
-                mm(b("k6", S_[8 + 4 * h:12 + 4 * h], S_[k::16]), b("sk", S_[2048 * h + k:2048 * h + 2048:16]), b("B8s"), True, True)
-        act(b("st"), b("k6", S_[8:16]))
+        act(b("bU"), bG)
+        stakes(0)
         for j, p in enumerate(order):
             if j == 2:
                 mm(hd, b("Iw"), b("hR"), True, False)
@@ -555,9 +578,8 @@ def rank_program(g, core, T, topo):
             win_acc(p, j == 7)
             if j + 4 < 8:
                 win_feed(order[j + 4])
-        vt(b("el"), b("st"), b("k6", S_[0:8]), A.is_gt)
         for kk in (0, 1):
-            mm(b("k6", full, S_[kk::2]), b("I"), b("xb"), True, True)
+            mm(b("k2", full, S_[kk::2]), b("I"), b("xb"), True, True)
         for h in (0, 1):
             mm(b("k7", S_[128 * h:128 * h + 128]), b("xb", S_[128 * h:128 * h + 128]), b("BlkV"), False, False)
         forder = mix(NV["far"])
@@ -565,7 +587,7 @@ def rank_program(g, core, T, topo):
         def far_feed(p):
             o = b("mR", S_[512 * p:512 * p + 512])
             if p < NV["far"]:
-                vt(o, b("xk", S_[p::8]), b("k6"), A.min)
+                vt(o, b("xk", S_[p::8]), b("k2"), A.min)
             else:
                 bk = sbank()
                 mm(b(bk), b("I"), b("xk", S_[p::8]), True, False)
@@ -583,10 +605,19 @@ def rank_program(g, core, T, topo):
             far_feed(p)
         for h in (0, 1):
             mm(b("k1", S_[4 * h:4 * h + 4]), b("gt", S_[128 * h:128 * h + 128]), b("Blk"), True, True)
-        mm(b("k2", S_[0:8]), b("Blk"), b("gt"), True, True)
+        mm(b("k1", S_[8:16]), b("Blk"), b("gt"), True, True)
         far_feed(forder[2])
+        stakes(1)
+        act(b("st"), b("k6", S_[8:16]), F.Sign)
+        mm(b("k6", S_[0:8]), b("zer", S_[0:128]), b("zer"), True, False)
+        for h in (0, 1):
+            mm(b("k6", S_[4 * h:4 * h + 4]), b("mine", S_[128 * h:128 * h + 128]), b("nI"), False, False)
+        vs(b("wl"), b("k1", S_[0:8]), b("Z"), A.is_ge)
+        mm(b("k6", S_[0:8]), b("I"), b("st"), False, False)
+        mm(b("k6", S_[0:8]), b("I"), b("wl"), False, True)
+        act(b("elw"), b("k6", S_[0:8]), F.Relu, bias=-1.0)
         vt(hd, b("hU"), hd, A.add)
-        vs(b("winG"), b("k2", S_[0:8]), b("Z"), A.is_ge)
+        vs(b("winG"), b("k1", S_[8:16]), b("Z"), A.is_ge)
         vt(hd, b("winG"), hd, A.mult)
         CN = "CN%d" % t
         vt(b(CN), b("vHL%d" % t), hd, A.add)
@@ -596,18 +627,14 @@ def rank_program(g, core, T, topo):
                 send(b(CN), [(d, "lb%d%d" % (t, d), "b%d%d" % (t, d)) for d in ds[j:j + 2]], NE)
             vals(t + 1)
         vc(b("tab0", S_[t:2048:8]), b(CN))
-        far_feed(forder[3])
+        for p in forder[3:6]:
+            far_feed(p)
         for p in forder[:3]:
             far_acc(p, False)
         nxt = t < RO - 1
         goal = b("k5", full, S_[0:16])
-        mm(goal, b("I32"), b("dumG"), True, False)
         if nxt:
-            wrap("k2", "tab0", 0, 128)
-        for p in forder[4:6]:
-            far_feed(p)
-        vs(b("k1", S_[0:8]), b("k1", S_[0:8]), b("Z"), A.is_ge)
-        vt(b("elw"), b("el"), b("k1", S_[0:8]), A.mult)
+            wrap("k5", "tab0", 0, 128)
         for p in forder[3:5]:
             far_acc(p, False)
         for j in (6, 7):
@@ -620,7 +647,7 @@ def rank_program(g, core, T, topo):
             mm(b("k4", S_[4 * h:4 * h + 4]), b("FK", S_[128 * h:128 * h + 128]), b("I32"), True, True)
         act(b("FKk"), b("k4", S_[0:8]))
         if nxt:
-            unwrap("k2", "off0", 0, 128)
+            unwrap("k5", "off0", 0, 128)
             op("v", lambda: v.tensor_reduce(ap(b("cnw")), ap(b("winG")), AxisListType.X, A.add), [b("winG")], [b("cnw")])
         spread_max("fS", 1.0)
         if nxt:
@@ -630,12 +657,15 @@ def rank_program(g, core, T, topo):
             s_, u_ = NEXT[t][0] if t == 0 else 3, NEXT[t][1] if t == 0 else 6
             for d in (s_, u_):
                 act(b("tab%d" % d, S_[t:2048:8]), b("lb%d%d" % (t, d)))
-        vt(b("soh"), b("FKk"), b("k2", S_[0:8]), A.is_equal)
-        vt(b("ga"), b("soh"), b("aD"), A.mult)
+        mm(goal, b("I32"), b("dumG"), True, False)
+        vt(hot, b("FKk"), b("k2", S_[0:8]), A.is_equal)
+        vt(b("ga"), b("aD"), hot, A.mult)
         mm(goal, b("Blk32"), b("ga"), False, True)
-        vt(b("ca"), b("soh"), b("cK"), A.mult)
+        vt(b("ca"), b("cK"), hot, A.mult)
         csG = b("k6", S_[0:8])
         mm(csG, b("Blk32"), b("ca"), True, True)
+        mm(hd, b("I32"), b("vG%d" % t), True, True)
+        vt(b("sb"), b("bU"), hot, A.mult)
         if nxt:
             for h in (0, 1):
                 c1(s_, h, "s")
@@ -644,7 +674,7 @@ def rank_program(g, core, T, topo):
         vc(b("gSu"), goal)
         vc(b("go"), b("gws", S_[15::16]))
         act(b("OG"), ind(b("O", S_[:]), b("go")))
-        act(b("ns"), b("soh"), scale=-1.0, bias=1.0)
+        act(rest, hot, scale=-1.0, bias=1.0)
         dup = b("k4", full, S_[0:16])
         mm(dup, b("I"), b("zer"), True, False)
         for c in range(16):
@@ -654,28 +684,25 @@ def rank_program(g, core, T, topo):
             if nxt and c in (1, 6):
                 h = c // 6
                 wrap("k3", "T1", 64 * h, 64 * h + 64)
-            if nxt and c in (8, 13):
-                h = c // 13
+            if nxt and c in (13, 15):
+                h = c // 15
                 unwrap("k3", "off1", 64 * h, 64 * h + 64)
                 c2(u_, h, "s")
         vt(b("E3", full, S_[0:16]), b("E3", full, S_[0:16]), b("tri"), A.mult)
         mm(dup, b("B4096"), b("E3", full, S_[0:16]), False, True)
-        vt(b("eqv"), b("OG"), b("vG%d" % t), A.is_equal)
-        vt(b("dd"), csG, b("OG"), A.subtract)
-        vt(b("tt"), b("eqv"), b("dd"), A.mult)
+        vt(b("eqv"), b("OG"), hd, A.is_equal)
+        vt(csG, csG, b("OG"), A.subtract)
+        vt(b("tt"), b("eqv"), csG, A.mult)
         vt(b("dw"), dup, b("maskW"), A.mult)
         scan(b("dws"), b("rst"), b("dw"), A.mult, A.add)
         vt(b("t1"), b("dws", S_[15::16]), b("dumW"), A.min)
-        vt(b("sb"), b("soh"), bG, A.mult)
         vt(b("t2"), b("t1"), b("gws", S_[15::16]), A.max)
         vc(b("so"), b("t2"))
         vt(ind(b("O", S_[:]), b("so")), b("OG"), b("tt"), A.add)
         if not nxt:
             break
         vc(b("a16"), b("O", S_[t + 1:2048:8]))
-    t = RO - 1
-    vt(b("oc"), b("O", S_[t:2048:8]), b("ns"), A.mult)
-    vt(b("O", S_[t:2048:8]), b("oc"), b("sb"), A.add)
+    sellers(RO - 1)
     for j, bk in enumerate(("k1", "k2", "k3", "k4")):
         mm(b(bk), b("BlkC"), b("tab0", S_[512 * j:512 * j + 512]), True, True)
         act(b("ycS", S_[512 * j:512 * j + 512]), b(bk), bias=-2048.0)

import numpy as np
from concourse.mybir import AluOpType as A, ActivationFunctionType as F, AxisListType
from concourse.bass import DstId, RemoteDMATransfer

V, D, L, RO, N = 2048, 8, 256, 3, 8
DEL = (1, 2, 4, 3, 6)
NEXT = {0: (2, 4, 3, 6), 1: (3, 6)}
NV = {"min": 8, "win": 5, "far": 6, "d": 128, "sk": 2, "sk2": 0, "c0": 5, "c1": 0}
NA = 1
S_ = np.s_

_bf, _f, _i, _u = "bfloat16", "float32", "int32", "uint16"
_shapes = {
    "O": ([2304], _f), "holI": ([2048], _i), "X": ([2048], _bf), "raw": ([128], _i), "rawd": ([128], _f),
    "HL": ([256], _bf), "VV": ([4096], _f), "xk": ([4096], _bf), "sk": ([4096], _bf), "dR": ([4096], _bf),
    "mR": ([4096], _bf), "pR": ([4096], _bf), "T1": ([2048], _bf), "DT": ([2048], _bf), "EK": ([2048], _bf),
    "E3": ([16, 272], _bf), "ycS": ([2048], _f),
    "EQ": ([128, 16], _bf), "PA": ([128, 16], _bf), "PB": ([80, 32], _bf),
    "off0": ([128], _u), "off1": ([128], _u), "a16": ([256], _u), "bo": ([16], _u), "go": ([16], _u), "so": ([16], _u),
    "gSu": ([256], _u), "aD": ([256], _f), "cd": ([16, 24], _f), "md": ([16, 24], _bf), "cS": ([256], _f),
    "bU": ([256], _f), "keyS": ([256], _f), "mxS": ([256], _f), "keyK": ([256], _f), "mx16": ([128], _f), "ohc": ([256], _f),
    "cK": ([256], _f), "mine": ([256], _bf), "w1": ([256], _bf), "w16": ([256], _bf), "bw": ([256], _f), "bws": ([256], _f),
    "xb": ([256], _bf), "gt": ([256], _bf), "wl": ([256], _bf), "winG": ([256], _f), "st": ([256], _bf), "el": ([256], _f), "elw": ([256], _f),
    "FK": ([256], _f), "FKk": ([256], _f), "fS": ([256], _f), "ga": ([256], _f), "ca": ([256], _f), "ns": ([256], _f),
    "sb": ([256], _f), "gw": ([256], _f), "gws": ([256], _f), "OG": ([256], _f), "dw": ([256], _f), "dws": ([256], _f),
    "t1": ([16], _f), "t2": ([16], _f), "eqv": ([256], _f), "dd": ([256], _f), "tt": ([256], _f), "oc": ([256], _f),
    "hR": ([256], _bf), "hU": ([256], _f), "vR": ([256], _bf), "vW": ([256], _bf), "vU": ([256], _f),
    "cnw": ([1], _f), "cni": ([1], _i), "cnp": ([1], _i), "Z": ([1], _f),
    "IF": ([256], _f), "JG": ([256], _f), "JM": ([256], _f), "JM3": ([16, 16], _f), "pi": ([1], _i), "qi": ([1], _i),
    "cols": ([16], _f), "I": ([128], _bf), "I16": ([128], _bf), "I256": ([128], _bf), "nI": ([128], _bf), "Iw": ([128], _bf),
    "I32": ([128], _f), "Ip32": ([128], _f), "Blk": ([128], _bf), "Blk32": ([128], _f), "BlkC": ([128], _bf), "B4096": ([128], _bf), "BlkV": ([128], _bf),
    "fm": ([16, 8], _bf), "Blk8": ([8], _bf), "Blk8c": ([8], _bf), "B8s": ([8], _bf), "B816": ([8], _bf), "B8n32": ([8], _bf),
    "B8h": ([8], _bf), "B8nh": ([8], _bf), "KSc": ([144], _bf),
    "km": ([16], _f), "maskW": ([256], _f), "rst": ([256], _f), "tri": ([16, 16], _bf), "E1": ([256], _f), "k15": ([16, 16], _bf),
    "kc": ([256], _bf), "dumG": ([256], _f), "dumW": ([16], _f), "zer": ([256], _bf), "o16": ([128], _f),
}
SCRATCH = {n: ("sbuf", [128] + s, d) for n, (s, d) in _shapes.items()}
PACK = {n: 256 * j for j, n in enumerate((
    "aD cS keyS mxS keyK ohc cK bw bws el elw winG FK FKk fS ga ca bU sb gw gws OG dw dws eqv tt hU vU").split())}
SHAPE = dict(SCRATCH)
for _n in PACK:
    del SCRATCH[_n]
SCRATCH["lanes"] = ("sbuf", [128, 256 * len(PACK)], _f)
for _d in (0,) + DEL:
    SCRATCH["tab%d" % _d] = ("sbuf", [128, 2048], _bf)
for _d in DEL:
    SCRATCH["la%d" % _d] = ("sbuf", [128, 256], _bf)
for _t in NEXT:
    for _d in NEXT[_t]:
        SCRATCH["lb%d%d" % (_t, _d)] = ("sbuf", [128, 256], _bf)
for _t in range(RO):
    SCRATCH["CN%d" % _t] = ("sbuf", [128, 256], _bf)
    SCRATCH["vHL%d" % _t] = ("sbuf", [128, 256], _bf)
    SCRATCH["vG%d" % _t] = ("sbuf", [128, 256], _f)
for _k in range(8):
    SCRATCH["k%d" % _k] = ("psum", [128, 512] if _k in (0, 7) else [128, 16, 32], _f)
SHAPE.update(SCRATCH)
SEMAPHORES = ["qv", "qs", "qp", "qg", "ls"] + ["d%d" % k for k in range(24)] + ["a%d" % d for d in DEL] + ["b%d%d" % (t, d) for t in NEXT for d in NEXT[t]]


def b(n, *ix):
    return (n, (slice(None),) + ix)


def bp(n, p, *ix):
    return (n, (p,) + ix)


def ind(w, o):
    return ("ind", w, o)


def rank_program(g, core, T, topo):
    rank = T.rank_of(core)
    if rank is None:
        return
    eng = {"v": g.vector, "s": g.scalar, "p": g.tensor, "g": g, "y": g.sync}
    cnt, clk, hist, W, R, cache = {}, {q: {} for q in eng}, {}, {}, {}, {}
    ndma = [0]

    def ap(x):
        if x[0] == "ind":
            return T[x[1][0]][x[1][1]].indirect(T[x[2][0]][x[2][1]])
        if x[0] in PACK:
            lo, hi, st = (x[1][1] if len(x[1]) > 1 else slice(None)).indices(256)
            return T["lanes"][x[1][0], PACK[x[0]] + lo:PACK[x[0]] + hi:st]
        return T[x[0]][x[1]]

    def parts(xs):
        out = []
        for x in xs:
            if isinstance(x, tuple):
                out += [x[1], x[2]] if x[0] == "ind" else [x]
        return out

    def size(n):
        return int(np.prod(SHAPE[n][1][1:]))

    def cols(x):
        key = repr(x)
        if key not in cache:
            ix = x[1][1:]
            m = np.arange(size(x[0])).reshape(SHAPE[x[0]][1][1:])
            cache[key] = m[ix].ravel() if ix else m.ravel()
        return cache[key]

    def need(q, rd, wr):
        req = {}
        own = "q" + q

        def take(tab, x, skip):
            ps = SHAPE[x[0]][0] == "psum"
            for s, arr in tab.get(x[0], {}).items():
                if s == own and skip:
                    continue
                n = int(arr.max() if ps and s != own else arr[cols(x)].max())
                if n > req.get(s, 0):
                    req[s] = n
        for x in rd:
            take(W, x, False)
            if SHAPE[x[0]][0] == "psum":
                take(R, x, True)
        for x in wr:
            take(W, x, True)
            take(R, x, True)
        return req

    def waits(q, req):
        for s, n in sorted(req.items(), key=lambda z: -len(hist.get(z, ()))):
            if clk[q].get(s, 0) < n:
                eng[q].wait_ge(T.sem[s], n)
                clk[q][s] = n
                for s2, n2 in hist.get((s, n), {}).items():
                    clk[q][s2] = max(clk[q].get(s2, 0), n2)

    def note(tab, x, s, n):
        d = tab.setdefault(x[0], {})
        if s not in d:
            d[s] = np.zeros(size(x[0]), np.int64)
        d[s][cols(x)] = n

    def op(q, fn, rd, wr, sem=None, amt=1):
        rd, wr = parts(rd), parts(wr)
        waits(q, need(q, rd, wr))
        s = sem or "q" + q
        cnt[s] = cnt.get(s, 0) + amt
        n = cnt[s]
        fn().then_inc(T.sem[s], amt)
        hist[(s, n)] = dict(clk[q])
        if sem is None:
            hist[(s, n)][s] = n
        for x in rd:
            note(R, x, s, n)
        for x in wr:
            note(W, x, s, n)

    v, sc, te = g.vector, g.scalar, g.tensor

    def vt(out, i0, i1, o):
        op("v", lambda: v.tensor_tensor(ap(out), ap(i0), ap(i1), o), [i0, i1] + ([out[2]] if out[0] == "ind" else []), [out[1] if out[0] == "ind" else out])

    def vs(out, i0, s1, o1, s2=None, o2=None):
        a = [ap(x) if isinstance(x, tuple) else x for x in (s1, s2)]
        if o2 is None:
            op("v", lambda: v.tensor_scalar(ap(out), ap(i0), a[0], None, o1), [i0, s1], [out])
        else:
            op("v", lambda: v.tensor_scalar(ap(out), ap(i0), a[0], a[1], o1, o2), [i0, s1, s2], [out])

    def vc(out, i):
        op("v", lambda: v.tensor_copy(ap(out), ap(i)), [i], [out])

    def ms(out, c):
        op("v", lambda: v.memset(ap(out), c), [], [out])

    def scan(out, d0, d1, o0, o1):
        op("v", lambda: v.tensor_tensor_scan(ap(out), ap(d0), ap(d1), 0.0, o0, o1), [d0, d1], [out])

    def act(out, i, f=F.Identity, bias=0.0, scale=1.0):
        a = [ap(x) if isinstance(x, tuple) else x for x in (bias, scale)]
        op("s", lambda: sc.activation(ap(out), ap(i), f, bias=a[0], scale=a[1]), [i, bias, scale], [out])

    def mm(out, l, r, start, stop):
        op("p", lambda: te.matmul(ap(out), ap(l), ap(r), bool(start), bool(stop)), [l, r], [out])

    def iota(out, pat, base, cm):
        kw = {} if SCRATCH[out[0]][2] == _i else {"allow_small_or_imprecise_dtypes": True}
        op("g", lambda: g.iota(ap(out), pat, base, cm, **kw), [], [out])

    def dma(out, i):
        s = "d%d" % ndma[0]
        ndma[0] += 1
        o_, i_ = (ap(x) if x[0] in SCRATCH else T[x[0]][x[1]] for x in (out, i))
        op("y", lambda: g.sync.dma_start(o_, i_), [i] if i[0] in SCRATCH else [], [out] if out[0] in SCRATCH else [], s, 16)

    nls = [0]

    def send(src, items, ne):
        waits("g", need("g", [src], []))
        tr, k = [], 0
        for d, dst, sem in items:
            to = T.cores[(rank - d) % N]
            rid, pid = topo.addr(to)[:2]
            es = topo.engines(core, to)[k:k + ne]
            k += ne
            tr.append(RemoteDMATransfer(dst_ids=[DstId(rid=rid, pnc=pid)], dma_engine_mask=sum(1 << e for e in es), remote_sem=T.sem[sem], src=ap(src), dst=T[dst][:], alu_op=0))
            nls[0] += ne
        g.remote_dma_fused(tr, local_sem=T.sem.ls)

    def arrives(dst, sem, ne):
        cnt[sem] = ne
        note(W, b(dst), sem, ne)

    fills = []

    def fill(n=1):
        for _ in range(n):
            if fills:
                fills.pop(0)()
    full = S_[:]
    NE = 4
    dma(b("raw"), ("ctl", S_[:]))
    dma(b("holI"), ("hol", S_[:]))
    dma(b("X"), ("sha", S_[:]))
    iota(b("pi"), [[0, 1]], 0, 1)
    iota(b("IF"), [[1, 256]], 0, 0)
    iota(b("JG"), [[1, 16], [0, 16]], 0, 0)
    iota(b("JM"), [[0, 16], [1, 16]], 0, 0)
    col = {n: b("cols", S_[j:j + 1]) for j, n in enumerate(("p", "q", "g", "g15", "is", "po", "w", "po2"))}
    vs(b("qi"), b("pi"), 15, A.bitwise_and)
    vc(col["p"], b("pi"))
    vc(col["q"], b("qi"))
    vt(col["g15"], b("pi"), b("qi"), A.subtract)
    vs(b("cni"), b("qi"), 1, A.bitwise_and)
    vs(col["g"], col["g15"], 1.0 / 16, A.mult)
    vs(col["is"], col["q"], 2.0, A.is_lt)
    vc(col["po"], b("cni"))
    vs(col["g15"], col["g15"], 15.0, A.add)

    def eye(n, c):
        vs(b(n), b("IF", S_[0:128]), col["p"], A.is_equal, c, A.mult)

    def blk(n, c):
        vs(b(n), b("JG", S_[0:128]), col["g"], A.is_equal, c, A.mult)

    def b8(n, c):
        vs(b(n), b("IF", S_[0:8]), col["g"], A.is_equal, c, A.mult)
    blk("Blk", 1.0)
    vs(b("km"), b("IF", S_[0:16]), col["q"], A.is_equal)
    for k in range(16):
        act(b("EK", S_[128 * k:128 * k + 128]), b("Blk"), F.Copy, scale=b("km", S_[k:k + 1]))
    eye("I", 1.0)
    vs(b("HL", S_[0:128]), b("raw"), 2048.0, A.add)
    vt(b("rawd"), b("raw"), b("HL", S_[0:128]), A.subtract)
    vs(b("HL", S_[128:256]), b("rawd"), 2048.0, A.add)
    ms(b("tab0"), 0.0)
    send(b("HL"), [(1, "la1", "a1"), (2, "la2", "a2")], NE)
    send(b("HL"), [(4, "la4", "a4"), (3, "la3", "a3")], NE)
    send(b("HL"), [(6, "la6", "a6")], NE)
    for d in DEL:
        arrives("la%d" % d, "a%d" % d, NE)
    for t in NEXT:
        for d in NEXT[t]:
            arrives("lb%d%d" % (t, d), "b%d%d" % (t, d), NE)

    def expand(n, src):
        o = [bp(n, S_[h:128:16], S_[:]) for h in (0, 1)]
        waits("y", need("y", [b(src)], [o[0]]))
        for h in (0, 1):
            s = "d%d" % ndma[0]
            ndma[0] += 1
            cnt[s] = 16
            g.sync.dma_start(ap(o[h]), ap(b(src, S_[128 * h:128 * h + 128]))).then_inc(T.sem[s], 16)
            hist[(s, 16)] = dict(clk["y"])
            note(R, b(src), s, 16)
            note(W, o[h], s, 16)
    expand("tab0", "HL")
    vs(b("KSc", S_[0:143]), b("IF", S_[0:143]), col["g15"], A.is_equal, col["is"], A.mult)
    for d in (1, 2):
        ms(b("tab%d" % d), 0.0)
    expand("tab1", "la1")
    expand("tab2", "la2")
    vs(col["w"], col["po"], -2.0, A.mult, 1.0, A.add)
    vs(col["po2"], col["po"], 2048.0, A.mult)
    for n, o, c in (("nI", "I", -1.0), ("I16", "I", 16.0), ("I256", "I", 256.0), ("I32", "I", 1.0), ("Iw", "I", col["w"]), ("Ip32", "I", col["po"]), ("Blk32", "Blk", 1.0),
                    ("B4096", "Blk", 4096.0), ("BlkC", "Blk", col["is"])):
        act(b(n), b(o), F.Copy, scale=c)
    for n, c in (("Blk8", 1.0), ("Blk8c", col["is"]), ("B8h", 0.5), ("B8nh", -0.5)):
        b8(n, c)

    def hl_v(t):
        act(b("vR"), b("vG%d" % t), bias=2048.0)
        act(b("vU"), b("vG%d" % t), bias=2048.0)
        mm(b("k4", S_[0:8]), b("Iw"), b("vR"), True, False)
        mm(b("k4", S_[0:8]), b("Ip32"), b("vU"), False, True)
        act(b("vHL%d" % t), b("k4", S_[0:8]))

    def vals(t):
        iota(b("VV"), [[8, 256], [0, 16]], t, 0)

    def wrap(bank, src, lo, hi):
        bk = b(bank, S_[lo // 32:hi // 32])
        for q in range(16):
            mm(bk, b("KSc", S_[15 - q:143 - q]), b(src, S_[16 * lo + q:16 * hi:16]), q == 0, q == 15)

    def unwrap(bank, out, lo, hi):
        vs(b(out, S_[lo:hi]), b(bank, S_[lo // 32:hi // 32]), -2048.0, A.add)

    def gath(e, out, w, o):
        if e == "s":
            act(out, ind(w, o))
        else:
            vc(out, ind(w, o))

    def c1(s, h, e):
        gath(e, b("T1", S_[1024 * h:1024 * h + 1024]), b("tab%d" % s, S_[:]), b("off0", S_[64 * h:64 * h + 64]))

    def c2(u, h, e):
        gath(e, b("DT", S_[1024 * h:1024 * h + 1024]), b("tab%d" % u, S_[:]), b("off1", S_[64 * h:64 * h + 64]))

    def gather_d(lo, hi, e):
        gath(e, b("dR", S_[16 * lo:16 * hi]), b("DT", S_[:]), b("a16", S_[lo:hi]))

    def gather_x(h):
        gath("s", b("xk", S_[2048 * h:2048 * h + 2048]), b("X", S_[:]), b("a16", S_[128 * h:128 * h + 128]))

    def sk_piece(t, j):
        w = b("O", S_[0:2048]) if t else b("holI", S_[:])
        vt(b("sk", S_[512 * j:512 * j + 512]), ind(w, b("a16", S_[32 * j:32 * j + 32])), b("VV", S_[512 * j:512 * j + 512]), A.is_equal)

    def xv_mm(t):
        for k in (0, 1):
            mm(b("k0", S_[k::2]), b("I"), b("X", S_[t:2048:8]), True, True)

    def min_v(p):
        vt(b("mR", S_[512 * p:512 * p + 512]), b("xk", S_[p::8]), b("k0"), A.min)

    def min_s(t, p):
        bk = "k1" if p % 2 else "k2"
        mm(b(bk), b("I"), b("xk", S_[p::8]), True, False)
        for kk in (0, 1):
            mm(b(bk, full, S_[kk::2]), b("nI"), b("X", S_[t:2048:8]), False, kk)
        act(b("mR", S_[512 * p:512 * p + 512]), b(bk), F.Abs)

    def m_mm(t, p):
        for k in (p, p + 8):
            for h in (0, 1):
                l = b("mR", S_[512 * p + 256 * h + k // 8:512 * p + 256 * h + 256:2])
                for o in ((k, k + 16) if k < 8 else (k,)):
                    out = b("k5", S_[8 * h:8 * h + 8], o)
                    if p < NV["min"]:
                        mm(out, l, b("Blk8"), True, True)
                    else:
                        mm(out, b("xk", S_[2048 * h + k:2048 * h + 2048:16]), b("B8h"), True, False)
                        mm(out, b("X", S_[1024 * h + t:1024 * h + 1024:8]), b("B8h"), False, False)
                        mm(out, l, b("B8nh"), False, True)

    def spread_max(src, least, mid=None):
        mm(bp("k1", S_[0:16], S_[0:4]), b(src, S_[15::16]), b("I32"), True, True)
        vs(bp("mx16", S_[0:16], S_[:]), bp("k1", S_[0:16], S_[0:4], full), least, A.max)
        if mid:
            mid()
        for h in (0, 1):
            mm(b("k2", S_[4 * h:4 * h + 4]), bp("E1", S_[0:16], S_[128 * h:128 * h + 128]), bp("mx16", S_[0:16], S_[:]), True, True)

    rest = b("k7", S_[256:512])

    def sellers(t):
        vt(rest, b("O", S_[t:2048:8]), rest, A.mult)
        vt(b("O", S_[t:2048:8]), b("sb"), rest, A.add)

    ms(b("fm", full, S_[0:NV["far"]]), 16.0)
    ms(b("fm", full, S_[NV["far"]:8]), 0.0)
    ms(b("zer"), 0.0)
    ms(b("o16"), 1.0 / 16)
    ms(b("Z"), 9.0)
    ms(b("O", S_[2048:2304]), 0.0)
    vs(b("dumW"), b("IF", S_[0:16]), 16.0, A.mult, col["q"], A.add)
    vt(b("BlkV"), b("Blk"), b("fm"), A.mult)
    vs(b("dumW"), b("dumW"), 2048.0, A.add)
    vc(b("a16"), b("holI", S_[0:2048:8]))
    wrap("k3", "tab0", 0, 128)
    gather_x(0)
    unwrap("k3", "off0", 0, 128)
    vals(0)
    for t in range(RO):
        iota(b("vG%d" % t), [[8, 256]], t, 0)
    iota(b("JM3"), [[0, 16], [1, 16]], 0, 0)
    iota(b("k15"), [[0, 16], [-1, 16]], 15, 0)
    for n, c in (("B8s", 1.0 / 16), ("B816", 16.0), ("B8n32", -32.0)):
        b8(n, c)
    vs(b("rst"), b("JM"), 0.0, A.is_gt)
    vs(b("maskW"), b("JM"), col["q"], A.is_equal)
    vs(b("kc"), b("JM"), -1.0, A.mult, 31.0, A.add)
    vs(b("E1"), b("JG"), col["p"], A.is_equal)
    vs(b("dumG"), b("IF"), 2048.0, A.add)
    c1(1, 0, "s")
    c1(1, 1, "v")
    for j in range(3):
        vc(b("O", S_[512 * j:512 * j + 512]), b("holI", S_[512 * j:512 * j + 512]))
    gather_x(1)
    for h in (1, 0):
        wrap("k3", "T1", 64 * h, 64 * h + 64)
    xv_mm(0)
    for h in (1, 0):
        unwrap("k3", "off1", 64 * h, 64 * h + 64)
        c2(2, h, "v")
    gather_d(0, 128, "s")
    gather_d(128, 256, "v")
    vt(b("aD"), b("holI", S_[0:2048:8]), b("dumG"), A.subtract)
    fills.append(lambda: vs(b("tri"), b("JM3"), col["q"], A.is_gt))
    for j in range(3, 4):
        fills.append(lambda j=j: vc(b("O", S_[512 * j:512 * j + 512]), b("holI", S_[512 * j:512 * j + 512])))
    for d in (4, 3, 6):
        dma(b("tab%d" % d), b("tab0"))
        expand("tab%d" % d, "la%d" % d)

    for t in range(RO):
        if t:
            gather_x(0)
            gather_x(1)
            gather_d(NV["d"], 256, "v")
            sellers(t - 1)
            gather_d(0, NV["d"], "s")
            xv_mm(t)
            vs(b("Z"), b("cnp"), 9.0, A.add)
            for j in range(NV["sk"]):
                sk_piece(t, j)
            vt(b("aD"), b("O", S_[t:2048:8]), b("dumG"), A.subtract)
        fills[0:0] = [lambda j=j, t=t: sk_piece(t, j) for j in range(NV["sk"] if t else 0, 8)]
        for p in range(NV["min"]):
            min_v(p)
        if t:
            fill(NV["sk2"])
        for p in range(NV["min"], 8):
            min_s(t, p)

        def c_mm(h):
            for k in range(16):
                mm(b("k4", S_[8 * h:8 * h + 8], k), b("dR", S_[2048 * h + k:2048 * h + 2048:16]), b("Blk8c"), True, True)
        for p in range(8):
            if p == NV["c0"]:
                c_mm(0)
            if p == NV["c1"]:
                c_mm(1)
            m_mm(t, p)
        act(b("md"), b("k5", full, S_[0:24]))
        c4 = b("k4", full, S_[0:16])
        vc(b("cd", full, S_[0:16]), c4)
        vc(b("cd", full, S_[16:24]), b("k4", full, S_[0:8]))
        pool = b("k6", full, S_[0:16])
        mm(pool, b("I"), b("k15"), True, False)
        mm(pool, b("I16"), b("md", full, S_[0:16]), False, False)
        back = [(1, s) for s in range(1, 9 - NA)] + [x for s in range(9 - NA, 9) for x in ((1, s), (0, s)) if x != (1, 8)]
        for s in range(1, 9):
            eq = b("EQ", S_[16 * s - 16:16 * s], full)
            vt(eq, b("cd", full, S_[s:s + 16]), c4, A.is_equal)
            for j, (way, r) in enumerate(back):
                if r != s:
                    continue
                bank = "k1" if j // 2 % 2 == 0 else "k2"
                reg = b(bank, full, S_[16 * (j % 2):16 * (j % 2) + 16])
                mm(reg, b("I256"), eq, True, False)
                mm(reg, b("I"), b("md", full, S_[0:16] if way else S_[s:s + 16]), False, True)
                if j % 2:
                    act(b("PB", S_[8 * j - 8:8 * j + 8], full), b(bank, full, full), F.Relu, bias=-256.0)
        act(b("cS"), c4)

        def pool_b(j):
            way, s = back[j]
            z, o = S_[16 * (j // 2):16 * (j // 2) + 16], 16 * (j % 2)
            if way:
                mm(b("k6", full, S_[s:16]), b("I16"), b("PB", z, S_[o:o + 16 - s]), False, False)
                mm(b("k6", full, S_[0:s]), b("I16"), b("PB", z, S_[o + 16 - s:o + 16]), False, False)
            else:
                mm(pool, b("I16"), b("PB", z, S_[o:o + 16]), False, j == len(back) - 1)
        for s in range(1, 9 - NA):
            eq = b("EQ", S_[16 * s - 16:16 * s], full)
            vt(b("PA", S_[16 * s - 16:16 * s], full), eq, b("k5", full, S_[s:s + 16]), A.mult)
            mm(pool, b("I16"), b("PA", S_[16 * s - 16:16 * s], full), False, False)
            if s > 1:
                pool_b(s - 2)
        for j in range(7 - NA, len(back)):
            pool_b(j)
        fill(1)
        for h in (0, 1):
            mm(b("k3", S_[4 * h:4 * h + 4]), b("cS", S_[128 * h:128 * h + 128]), b("I32"), True, True)
        act(b("cK"), b("k3", S_[0:8]), bias=-2048.0)
        vc(b("keyS"), pool)
        scan(b("mxS"), b("rst"), b("keyS"), A.mult, A.max)
        for h in (0, 1):
            mm(b("k3", S_[8 + 4 * h:12 + 4 * h]), b("keyS", S_[128 * h:128 * h + 128]), b("I32"), True, True)
        act(b("keyK"), b("k3", S_[8:16]))
        fl = b("k7", S_[0:256])
        if t == 1:
            for d in (3, 6):
                act(b("tab%d" % d, S_[0:2048:8]), b("lb0%d" % d))
        fl = b("k7", S_[0:256])

        def far_const():
            mm(fl, b("I"), b("kc"), True, False)
            for p in range(NV["far"]):
                for k in (p, p + 8):
                    for h in (0, 1):
                        mm(b("k7", S_[128 * h + k:128 * h + 128:16]), b("xk", S_[2048 * h + k:2048 * h + 2048:16]), b("B816"), False, False)
        fill(1)
        spread_max("mxS", 0.0, lambda: fill(1))
        hl_v(t)

        def stakes(h):
            for k in range(16):
                mm(b("k6", S_[8 + 4 * h:12 + 4 * h], S_[k::16]), b("sk", S_[2048 * h + k:2048 * h + 2048:16]), b("B8s"), True, True)
        hot = b("k1", S_[8:16])
        vt(hot, b("keyK"), b("k2", S_[0:8]), A.is_equal)
        vt(b("ohc"), b("cK"), hot, A.mult)
        bG = b("k0", S_[0:256])
        mm(bG, b("Blk32"), b("ohc"), True, True)
        far_const()
        fill(1)
        vt(b("mine"), b("cK"), bG, A.is_equal)
        vs(b("w1"), b("mine"), 2.0, A.mult, -1.0, A.add)
        act(b("w16"), b("mine"), scale=32.0, bias=-16.0)
        vt(b("bw"), bG, b("maskW"), A.mult)
        scan(b("bws"), b("rst"), b("bw"), A.mult, A.add)
        vc(b("bo"), b("bws", S_[15::16]))
        dps = b("k5", S_[0:8])
        first = [True]
        nv, ns_ = [0], [0]

        def vbank():
            nv[0] += 1
            return "k1" if nv[0] % 2 else "k2"

        def sbank():
            ns_[0] += 1
            return "k4" if ns_[0] % 2 else "k3"

        def win_feed(p):
            vec = p < NV["win"]
            bk = vbank() if vec else sbank()
            if not vec:
                mm(b(bk), b("I"), b("xk", S_[p::8]), True, False)
            for kk in (0, 1):
                k = p + 8 * kk
                mm(b(bk, full, S_[kk::2]), b("EK", S_[128 * k:128 * k + 128]), b("w1" if vec else "w16"), vec, vec or kk)
            o = b("pR", S_[512 * p:512 * p + 512])
            if vec:
                vt(o, b("xk", S_[p::8]), b(bk), A.mult)
            else:
                act(o, b(bk), F.Abs)

        def win_acc(p, last):
            for kk in (0, 1):
                mm(dps, b("I"), b("pR", S_[512 * p + kk:512 * p + 512:2]), first[0], last and kk)
                first[0] = False

        def mix(nv_):
            vps, sps = list(range(nv_)), list(range(nv_, 8))
            out = []
            for j in range(8):
                out += vps[j:j + 1] + sps[j:j + 1]
            return out
        order = mix(NV["win"])
        for p in order[:2]:
            win_feed(p)
        fill(99)
        for p in order[2:4]:
            win_feed(p)
        act(b("xb"), ind(b("X", S_[:]), b("bo")))
        hd = b("k0", S_[256:512])
        act(b("hR"), bG, bias=2048.0)
        act(b("hU"), bG, bias=col["po2"], scale=col["po"])
        act(b("bU"), bG)
        stakes(0)
        for j, p in enumerate(order):
            if j == 2:
                mm(hd, b("Iw"), b("hR"), True, False)
                mm(hd, b("nI"), b("vHL%d" % t), False, True)
            win_acc(p, j == 7)
            if j + 4 < 8:
                win_feed(order[j + 4])
        for kk in (0, 1):
            mm(b("k2", full, S_[kk::2]), b("I"), b("xb"), True, True)
        for h in (0, 1):
            mm(b("k7", S_[128 * h:128 * h + 128]), b("xb", S_[128 * h:128 * h + 128]), b("BlkV"), False, False)
        forder = mix(NV["far"])

        def far_feed(p):
            o = b("mR", S_[512 * p:512 * p + 512])
            if p < NV["far"]:
                vt(o, b("xk", S_[p::8]), b("k2"), A.min)
            else:
                bk = sbank()
                mm(b(bk), b("I"), b("xk", S_[p::8]), True, False)
                for kk in (0, 1):
                    mm(b(bk, full, S_[kk::2]), b("nI"), b("xb"), False, kk)
                act(o, b(bk), F.Abs)

        def far_acc(p, last):
            for k in (p, p + 8):
                for h in (0, 1):
                    mm(b("k7", S_[128 * h + k:128 * h + 128:16]), b("mR", S_[512 * p + 256 * h + k // 8:512 * p + 256 * h + 256:2]),
                       b("B8n32" if p < NV["far"] else "B816"), False, last and k > 7 and h)
        vs(b("gt"), dps, 32.0 * (8 - NV["win"]), A.is_gt)
        for p in forder[:2]:
            far_feed(p)
        for h in (0, 1):
            mm(b("k1", S_[4 * h:4 * h + 4]), b("gt", S_[128 * h:128 * h + 128]), b("Blk"), True, True)
        mm(b("k1", S_[8:16]), b("Blk"), b("gt"), True, True)
        far_feed(forder[2])
        stakes(1)
        act(b("st"), b("k6", S_[8:16]), F.Sign)
        mm(b("k6", S_[0:8]), b("zer", S_[0:128]), b("zer"), True, False)
        for h in (0, 1):
            mm(b("k6", S_[4 * h:4 * h + 4]), b("mine", S_[128 * h:128 * h + 128]), b("nI"), False, False)
        vs(b("wl"), b("k1", S_[0:8]), b("Z"), A.is_ge)
        mm(b("k6", S_[0:8]), b("I"), b("st"), False, False)
        mm(b("k6", S_[0:8]), b("I"), b("wl"), False, True)
        act(b("elw"), b("k6", S_[0:8]), F.Relu, bias=-1.0)
        vt(hd, b("hU"), hd, A.add)
        vs(b("winG"), b("k1", S_[8:16]), b("Z"), A.is_ge)
        vt(hd, b("winG"), hd, A.mult)
        CN = "CN%d" % t
        vt(b(CN), b("vHL%d" % t), hd, A.add)
        if t in NEXT:
            ds = NEXT[t]
            for j in range(0, len(ds), 2):
                send(b(CN), [(d, "lb%d%d" % (t, d), "b%d%d" % (t, d)) for d in ds[j:j + 2]], NE)
            vals(t + 1)
        vc(b("tab0", S_[t:2048:8]), b(CN))
        for p in forder[3:6]:
            far_feed(p)
        for p in forder[:3]:
            far_acc(p, False)
        nxt = t < RO - 1
        goal = b("k5", full, S_[0:16])
        if nxt:
            wrap("k5", "tab0", 0, 128)
        for p in forder[3:5]:
            far_acc(p, False)
        for j in (6, 7):
            far_feed(forder[j])
        for j in (5, 6, 7):
            far_acc(forder[j], j == 7)
        vt(b("FK"), b("elw"), fl, A.mult)
        scan(b("fS"), b("rst"), b("FK"), A.mult, A.max)
        for h in (0, 1):
            mm(b("k4", S_[4 * h:4 * h + 4]), b("FK", S_[128 * h:128 * h + 128]), b("I32"), True, True)
        act(b("FKk"), b("k4", S_[0:8]))
        if nxt:
            unwrap("k5", "off0", 0, 128)
            op("v", lambda: v.tensor_reduce(ap(b("cnw")), ap(b("winG")), AxisListType.X, A.add), [b("winG")], [b("cnw")])
        spread_max("fS", 1.0)
        if nxt:
            mm(b("k3", 15, S_[31:32]), b("o16"), b("cnw"), True, True)
            vc(b("cni"), b("k3", 15, S_[31:32]))
            vs(b("cnp"), b("cni"), 1, A.bitwise_and)
            s_, u_ = NEXT[t][0] if t == 0 else 3, NEXT[t][1] if t == 0 else 6
            for d in (s_, u_):
                act(b("tab%d" % d, S_[t:2048:8]), b("lb%d%d" % (t, d)))
        mm(goal, b("I32"), b("dumG"), True, False)
        vt(hot, b("FKk"), b("k2", S_[0:8]), A.is_equal)
        vt(b("ga"), b("aD"), hot, A.mult)
        mm(goal, b("Blk32"), b("ga"), False, True)
        vt(b("ca"), b("cK"), hot, A.mult)
        csG = b("k6", S_[0:8])
        mm(csG, b("Blk32"), b("ca"), True, True)
        mm(hd, b("I32"), b("vG%d" % t), True, True)
        vt(b("sb"), b("bU"), hot, A.mult)
        if nxt:
            for h in (0, 1):
                c1(s_, h, "s")
        vt(b("gw"), goal, b("maskW"), A.mult)
        scan(b("gws"), b("rst"), b("gw"), A.mult, A.add)
        vc(b("gSu"), goal)
        vc(b("go"), b("gws", S_[15::16]))
        act(b("OG"), ind(b("O", S_[:]), b("go")))
        act(rest, hot, scale=-1.0, bias=1.0)
        dup = b("k4", full, S_[0:16])
        mm(dup, b("I"), b("zer"), True, False)
        for c in range(16):
            vs(b("E3", c, S_[0:256 - 16 * c]), b("gSu", S_[16 * c:256]), b("gws", S_[16 * c + 15:16 * c + 16]), A.is_equal)
            if c < 15:
                mm(b("k4", S_[c + 1:16], S_[0:16]), b("B4096"), b("E3", c, S_[16:256 - 16 * c]), False, False)
            if nxt and c in (1, 6):
                h = c // 6
                wrap("k3", "T1", 64 * h, 64 * h + 64)
            if nxt and c in (13, 15):
                h = c // 15
                unwrap("k3", "off1", 64 * h, 64 * h + 64)
                c2(u_, h, "s")
        vt(b("E3", full, S_[0:16]), b("E3", full, S_[0:16]), b("tri"), A.mult)
        mm(dup, b("B4096"), b("E3", full, S_[0:16]), False, True)
        vt(b("eqv"), b("OG"), hd, A.is_equal)
        vt(csG, csG, b("OG"), A.subtract)
        vt(b("tt"), b("eqv"), csG, A.mult)
        vt(b("dw"), dup, b("maskW"), A.mult)
        scan(b("dws"), b("rst"), b("dw"), A.mult, A.add)
        vt(b("t1"), b("dws", S_[15::16]), b("dumW"), A.min)
        vt(b("t2"), b("t1"), b("gws", S_[15::16]), A.max)
        vc(b("so"), b("t2"))
        vt(ind(b("O", S_[:]), b("so")), b("OG"), b("tt"), A.add)
        if not nxt:
            break
        vc(b("a16"), b("O", S_[t + 1:2048:8]))
    sellers(RO - 1)
    for j, bk in enumerate(("k1", "k2", "k3", "k4")):
        mm(b(bk), b("BlkC"), b("tab0", S_[512 * j:512 * j + 512]), True, True)
        act(b("ycS", S_[512 * j:512 * j + 512]), b(bk), bias=-2048.0)
    dma(("yo", S_[:]), b("O", S_[0:2048]))
    dma(("yc", S_[:]), bp("ycS", S_[0:128:16], S_[:]))
    for s, n in cnt.items():
        g.wait_ge(T.sem[s], n)
    g.wait_ge(T.sem.ls, nls[0])
